import numpy as np
import ml_dtypes


def mxq(x, axis, fmt="e4m3"):
    dtype, down = {"e4m3": (ml_dtypes.float8_e4m3fn, 7), "e5m2": (ml_dtypes.float8_e5m2, 14)}[fmt]
    v = np.moveaxis(np.asarray(x, np.float32).astype(ml_dtypes.bfloat16).astype(np.float64), axis, -1)
    blocks = v.reshape(v.shape[:-1] + (-1, 32))
    amax = np.abs(blocks).max(-1, keepdims=True)
    byte = np.maximum(np.where(amax > 0, np.frexp(amax)[1] - 1 + 127, 0) - down, 1)
    scale = np.exp2(byte - 127.0)
    codes = (blocks / scale).astype(np.float32).astype(dtype).astype(np.float64)
    return np.moveaxis((codes * scale).reshape(v.shape), -1, axis)


WIDE = False


def mx_kscale(k):
    if not WIDE:
        return np.ones(k)
    levels = np.array([10, -10, 5, -5, 0])
    if k % 512:
        return np.exp2(np.random.permutation(np.resize(levels, k // 32))).repeat(32)
    a = np.empty((k // 512, 16))
    for p in range(k // 512):
        a[p, :8] = np.random.permutation(np.resize(levels, 8))
        for g in range(8):
            far = levels[np.abs(levels - a[p, g]) >= 10]
            a[p, g + 8] = far[np.random.randint(len(far))]
    return np.exp2(a.ravel()).repeat(32)


def f64(x):
    return np.asarray(x).astype(np.float64)


def striped(idx):
    return np.tile(idx.reshape(-1, 16).T, (8, 1)).astype(np.uint16)


def unstriped(offs):
    return offs[:16].T.reshape(-1).astype(np.int64)


E2M1 = np.array([0.0, 0.5, 1.0, 1.5, 2.0, 3.0, 4.0, 6.0, -0.0, -0.5, -1.0, -1.5, -2.0, -3.0, -4.0, -6.0])


def pack_fp4(w):
    k, n = w.shape
    w = f64(np.asarray(w, np.float32).astype(ml_dtypes.bfloat16)).reshape(k // 32, 32, n)
    amax = np.abs(w).max(1)
    mant, ex = np.frexp(amax / 6.0)
    byte = np.clip(np.where(amax > 0, np.where(mant > 0.5, ex, ex - 1) + 127, 1), 1, 254)
    scaled = (w * np.exp2(127.0 - byte)[:, None, :]).reshape(k, n).astype(np.float32)
    c = np.ascontiguousarray(scaled.reshape(k // 512, 128, 4, n).transpose(0, 1, 3, 2)).astype(ml_dtypes.float4_e2m1fn).view(np.uint8) & 0xF
    words = (c[..., 0::2] | (c[..., 1::2] << 4)).reshape(k // 512, 128, 2 * n)
    return np.ascontiguousarray(words), np.ascontiguousarray(byte.astype(np.uint8).reshape(k // 512, 16, n))


def unpack_fp4(words, scales):
    g, _, n = scales.shape
    words = np.ascontiguousarray(words).reshape(g, 128, n, 2)
    nib = np.empty((g, 128, n, 4), np.uint8)
    nib[..., 0::2] = words & 0xF
    nib[..., 1::2] = words >> 4
    vals = E2M1[nib] * np.repeat(np.exp2(scales.astype(np.float64) - 127.0), 8, axis=1)[..., None]
    return vals.transpose(0, 1, 3, 2).reshape(g * 512, n)


def sigmoid(v):
    return 1.0 / (1.0 + np.exp(-np.maximum(v, -700.0)))


K, T, S, V, N = 1024, 1024, 512, 256, 256


def setup_inputs():
    n = np.random.standard_normal
    s = mx_kscale(K)[:, None]
    packed_w1 = pack_fp4(n((K, N)) / np.sqrt(K) / s)
    return {
        "xT": (n((K, T)) * s).astype(np.float32),
        "w1_words": packed_w1[0],
        "w1_scales": packed_w1[1],
        "offs": striped(np.random.permutation(T)[:S]),
        "win": striped(np.random.permutation(S)[:V]),
        "lose": striped(np.random.permutation(S)[:V]),
    }


def reference(xT, w1_words, w1_scales, offs, win, lose):
    xq = mxq(f64(xT)[:, unstriped(offs)], 0, "e4m3")
    y = unpack_fp4(w1_words, w1_scales).T @ xq
    return sigmoid(y[:, unstriped(win)] - y[:, unstriped(lose)])

@@ -1,0 +1,156 @@
+from contextlib import ExitStack
+
+import concourse.mybir as mybir
+
+K, T, S, V, N = 1024, 1024, 512, 256, 256
+FLOPS = 2 * K * N * S
+
+F32 = mybir.dt.float32
+BF16 = mybir.dt.bfloat16
+I32 = mybir.dt.int32
+U32 = mybir.dt.uint32
+U16 = mybir.dt.uint16
+U8 = mybir.dt.uint8
+FP8X4 = mybir.dt.float8_e4m3fn_x4
+FP4X4 = mybir.dt.float4_e2m1fn_x4
+SIGMOID = mybir.ActivationFunctionType.Sigmoid
+SUBTRACT = mybir.AluOpType.subtract
+
+P = 128
+PASSES = K // 512
+GROUP = 128
+LIST_ROWS = 16
+
+LOADS = [
+    [(0, 512, 0), (512, 1024, 336)],
+    [(0, 512, 0), (512, 1024, 336)],
+    [(0, 512, 0), (512, 1024, 256)],
+    [(0, 512, 0), (512, 896, 384), (896, 1024, 0)],
+]
+PIECES = [[(0, 512)], [(0, 256), (256, 384), (384, 512)]]
+
+
+def tile_picked_ranknet_sigmoid_e_kernel(tc, xT, w1_words, w1_scales, offs, win, lose, out):
+    nc = tc.nc
+    x_rows = xT.rearrange("(z p j) t -> z p j t", p=P, j=4)
+
+    with ExitStack() as ctx:
+        keep = ctx.enter_context(tc.tile_pool(name="keep", bufs=1))
+        psum = ctx.enter_context(tc.psum_pool(name="psum", bufs=1))
+
+        offs_sb = keep.tile([P, S // LIST_ROWS], U16, name="offs_sb")
+        win_sb = keep.tile([P, V // LIST_ROWS], U16, name="win_sb")
+        lose_sb = keep.tile([P, V // LIST_ROWS], U16, name="lose_sb")
+
+        warm_in = keep.tile([P, 8], F32, name="warm_in")
+        warm_out = keep.tile([P, 8], F32, name="warm_out")
+        nc.vector.memset(warm_in[:], 0.0)
+        nc.scalar.activation(warm_out[:], warm_in[:], SIGMOID)
+
+        w_scales = keep.tile([P, PASSES, N], U8, name="w_scales", align_bytes=64)
+        nc.gpsimd.memset(w_scales[:].rearrange("p z n -> p (z n)").bitcast(I32), 0)
+        for q in range(4):
+            nc.gpsimd.dma_start(
+                out=w_scales[32 * q : 32 * q + 4].bitcast(I32),
+                in_=w1_scales[:, 4 * q : 4 * q + 4, :].rearrange("z r n -> r z n").bitcast(I32),
+            )
+
+        w_words = [keep.tile([P, 2 * N], U8, name="w_words%d" % z, align_bytes=64) for z in range(PASSES)]
+
+        raw = {}
+        for pair in range(2 * PASSES):
+            z, u = divmod(pair, 2)
+            for c0, c1, by_vector in LOADS[pair]:
+                raw[pair, c0] = keep.tile([P, 2, c1 - c0], F32, name="raw%d_%d" % (pair, c0))
+                nc.sync.dma_start(out=raw[pair, c0][:], in_=x_rows[z, :, 2 * u : 2 * u + 2, c0:c1])
+                if (pair, c0) == (0, 0):
+                    nc.sync.dma_start(offs_sb[:], offs)
+            if pair == 1:
+                nc.sync.dma_start(out=w_words[0][:], in_=w1_words[0])
+        nc.sync.dma_start(out=w_words[1][:], in_=w1_words[1])
+        nc.sync.dma_start(win_sb[:], win)
+        nc.sync.dma_start(lose_sb[:], lose)
+
+        banks = {}
+        for g in range(S // GROUP):
+            for b in range(N // P):
+                banks[g, b] = psum.tile([P, GROUP], F32, name="bank%d_%d" % (g, b))
+        y = [keep.tile([P, S], F32, name="y%d" % b) for b in range(N // P)]
+
+        def cast(pair):
+            window = keep.tile([P, 2 * T], BF16, name="window%d" % pair, align_bytes=64)
+            for c0, c1, by_vector in LOADS[pair]:
+                src = raw[pair, c0][:].rearrange("p e c -> p c e")
+                dst = window[:, 2 * c0 : 2 * c1].rearrange("p (c e) -> p c e", e=2)
+                by_scalar = c1 - c0 - by_vector
+                if by_scalar:
+                    nc.scalar.copy(dst[:, :by_scalar, :], src[:, :by_scalar, :])
+                if by_vector:
+                    nc.vector.tensor_copy(dst[:, by_scalar:, :], src[:, by_scalar:, :])
+            return window
+
+        def gather(window, u, picked, s0, s1):
+            words = picked[:].bitcast(U32).rearrange("p (s u) -> p s u", u=2)
+            nc.vector.tensor_copy(
+                words[:, :, u],
+                window[:].bitcast(U32).indirect(offs_sb[:, s0 // LIST_ROWS : s1 // LIST_ROWS]),
+            )
+
+        def multiply(z, picked, s0, s1):
+            codes = keep.tile([P, s1 - s0], U32, name="codes%d_%d" % (z, s0), align_bytes=64)
+            scales = keep.tile([P, s1 - s0], U8, name="scales%d_%d" % (z, s0), align_bytes=64)
+            nc.vector.quantize_mx(out=codes[:].bitcast(FP8X4), scales=scales[:], in_=picked[:])
+            for c in range(0, s1 - s0, GROUP):
+                g = (s0 + c) // GROUP
+                for b in range(N // P):
+                    nc.tensor.matmul_mx(
+                        out=banks[g, b][:],
+                        lhsT=w_words[z][:, 2 * P * b : 2 * P * (b + 1)].bitcast(FP4X4),
+                        lhsT_scale=w_scales[:, z, P * b : P * (b + 1)],
+                        rhs=codes[:, c : c + GROUP].bitcast(FP8X4),
+                        rhs_scale=scales[:, c : c + GROUP],
+                        start=(z == 0),
+                        stop=(z == PASSES - 1),
+                    )
+                    if z == PASSES - 1:
+                        nc.scalar.copy(y[b][:, GROUP * g : GROUP * (g + 1)], banks[g, b][:])
+
+        for z in range(PASSES):
+            pieces = PIECES[z]
+            picked = [
+                keep.tile([P, 4 * (s1 - s0)], BF16, name="picked%d_%d" % (z, s0), align_bytes=64)
+                for s0, s1 in pieces
+            ]
+            window = cast(2 * z)
+            for i, (s0, s1) in enumerate(pieces):
+                gather(window, 0, picked[i], s0, s1)
+            window = cast(2 * z + 1)
+            for i in range(len(pieces) + 1):
+                if i < len(pieces):
+                    gather(window, 1, picked[i], *pieces[i])
+                if i > 0:
+                    multiply(z, picked[i - 1], *pieces[i - 1])
+
+        won = [keep.tile([P, V], F32, name="won%d" % b) for b in range(N // P)]
+        lost = [keep.tile([P, V], F32, name="lost%d" % b) for b in range(N // P)]
+        margin = [keep.tile([P, V], F32, name="margin%d" % b) for b in range(N // P)]
+        result = [keep.tile([P, V], F32, name="result%d" % b) for b in range(N // P)]
+
+        def fetch(dst, b, places, v0, v1):
+            nc.vector.tensor_copy(dst[b][:, v0:v1], y[b][:].indirect(places[:, v0 // LIST_ROWS : v1 // LIST_ROWS]))
+
+        def compare(b, v0, v1):
+            nc.vector.tensor_tensor(margin[b][:, v0:v1], won[b][:, v0:v1], lost[b][:, v0:v1], SUBTRACT)
+            nc.scalar.activation(result[b][:, v0:v1], margin[b][:, v0:v1], SIGMOID)
+
+        half = V // 2
+        fetch(won, 0, win_sb, 0, V)
+        fetch(lost, 0, lose_sb, 0, V)
+        fetch(won, 1, win_sb, 0, V)
+        compare(0, 0, V)
+        nc.sync.dma_start(out=out[0:P, :], in_=result[0][:])
+        fetch(lost, 1, lose_sb, 0, half)
+        fetch(lost, 1, lose_sb, half, V)
+        compare(1, 0, half)
+        compare(1, half, V)
+        nc.sync.dma_start(out=out[P : 2 * P, :], in_=result[1][:])

@@ -22,12 +22,11 @@ GROUP = 128
 LIST_ROWS = 16
 
 LOADS = [
-    [(0, 512, 0), (512, 1024, 336)],
-    [(0, 512, 0), (512, 1024, 336)],
+    [(0, 1024, 656)],
+    [(0, 1024, 512)],
+    [(0, 512, 0), (512, 1024, 0)],
     [(0, 512, 0), (512, 1024, 256)],
-    [(0, 512, 0), (512, 896, 384), (896, 1024, 0)],
 ]
-PIECES = [[(0, 512)], [(0, 256), (256, 384), (384, 512)]]
 
 
 def tile_picked_ranknet_sigmoid_e_kernel(tc, xT, w1_words, w1_scales, offs, win, lose, out):
@@ -71,11 +70,12 @@ def tile_picked_ranknet_sigmoid_e_kernel(tc, xT, w1_words, w1_scales, offs, win,
         nc.sync.dma_start(win_sb[:], win)
         nc.sync.dma_start(lose_sb[:], lose)
 
-        banks = {}
-        for g in range(S // GROUP):
-            for b in range(N // P):
-                banks[g, b] = psum.tile([P, GROUP], F32, name="bank%d_%d" % (g, b))
+        groups = S // GROUP
+        banks = [psum.tile([P, GROUP], F32, name="bank%d" % g) for g in range(groups)]
+        wide_bank = psum.tile([P, S], F32, name="wide_bank")
         y = [keep.tile([P, S], F32, name="y%d" % b) for b in range(N // P)]
+        codes = [keep.tile([P, S], U32, name="codes%d" % z, align_bytes=64) for z in range(PASSES)]
+        scales = [keep.tile([P, S], U8, name="scales%d" % z, align_bytes=64) for z in range(PASSES)]
 
         def cast(pair):
             window = keep.tile([P, 2 * T], BF16, name="window%d" % pair, align_bytes=64)
@@ -87,49 +87,53 @@ def tile_picked_ranknet_sigmoid_e_kernel(tc, xT, w1_words, w1_scales, offs, win,
                     nc.scalar.copy(dst[:, :by_scalar, :], src[:, :by_scalar, :])
                 if by_vector:
                     nc.vector.tensor_copy(dst[:, by_scalar:, :], src[:, by_scalar:, :])
-            return window
+            return window[:].bitcast(U32)
 
-        def gather(window, u, picked, s0, s1):
-            words = picked[:].bitcast(U32).rearrange("p (s u) -> p s u", u=2)
-            nc.vector.tensor_copy(
-                words[:, :, u],
-                window[:].bitcast(U32).indirect(offs_sb[:, s0 // LIST_ROWS : s1 // LIST_ROWS]),
+        def entries(places, first, last):
+            return places[:, first // LIST_ROWS : last // LIST_ROWS]
+
+        def quantise(z, picked, s0, s1):
+            nc.vector.quantize_mx(out=codes[z][:, s0:s1].bitcast(FP8X4), scales=scales[z][:, s0:s1], in_=picked[:])
+
+        def multiply(bank, z, b, s0, s1):
+            nc.tensor.matmul_mx(
+                out=bank[:],
+                lhsT=w_words[z][:, 2 * P * b : 2 * P * (b + 1)].bitcast(FP4X4),
+                lhsT_scale=w_scales[:, z, P * b : P * (b + 1)],
+                rhs=codes[z][:, s0:s1].bitcast(FP8X4),
+                rhs_scale=scales[z][:, s0:s1],
+                start=(z == 0),
+                stop=(z == PASSES - 1),
             )
 
-        def multiply(z, picked, s0, s1):
-            codes = keep.tile([P, s1 - s0], U32, name="codes%d_%d" % (z, s0), align_bytes=64)
-            scales = keep.tile([P, s1 - s0], U8, name="scales%d_%d" % (z, s0), align_bytes=64)
-            nc.vector.quantize_mx(out=codes[:].bitcast(FP8X4), scales=scales[:], in_=picked[:])
-            for c in range(0, s1 - s0, GROUP):
-                g = (s0 + c) // GROUP
-                for b in range(N // P):
-                    nc.tensor.matmul_mx(
-                        out=banks[g, b][:],
-                        lhsT=w_words[z][:, 2 * P * b : 2 * P * (b + 1)].bitcast(FP4X4),
-                        lhsT_scale=w_scales[:, z, P * b : P * (b + 1)],
-                        rhs=codes[:, c : c + GROUP].bitcast(FP8X4),
-                        rhs_scale=scales[:, c : c + GROUP],
-                        start=(z == 0),
-                        stop=(z == PASSES - 1),
-                    )
-                    if z == PASSES - 1:
-                        nc.scalar.copy(y[b][:, GROUP * g : GROUP * (g + 1)], banks[g, b][:])
+        spans = [(GROUP * g, GROUP * (g + 1)) for g in range(groups)]
 
-        for z in range(PASSES):
-            pieces = PIECES[z]
-            picked = [
-                keep.tile([P, 4 * (s1 - s0)], BF16, name="picked%d_%d" % (z, s0), align_bytes=64)
-                for s0, s1 in pieces
-            ]
-            window = cast(2 * z)
-            for i, (s0, s1) in enumerate(pieces):
-                gather(window, 0, picked[i], s0, s1)
-            window = cast(2 * z + 1)
-            for i in range(len(pieces) + 1):
-                if i < len(pieces):
-                    gather(window, 1, picked[i], *pieces[i])
-                if i > 0:
-                    multiply(z, picked[i - 1], *pieces[i - 1])
+        picked = keep.tile([P, 4 * S], BF16, name="picked_first", align_bytes=64)
+        picked_words = picked[:].bitcast(U32).rearrange("p (s u) -> p s u", u=2)
+        for u in range(2):
+            nc.vector.tensor_copy(picked_words[:, :, u], cast(u).indirect(offs_sb[:]))
+        quantise(0, picked, 0, S)
+        for g, span in enumerate(spans):
+            multiply(banks[g], 0, 0, *span)
+        multiply(wide_bank, 0, 1, 0, S)
+
+        halves = [keep.tile([P, 2, GROUP], U32, name="halves%d" % g) for g in range(groups)]
+        woven = [keep.tile([P, 4 * GROUP], BF16, name="woven%d" % g, align_bytes=64) for g in range(groups)]
+        for u in range(2):
+            window = cast(2 + u)
+            for g, span in enumerate(spans):
+                nc.vector.tensor_copy(halves[g][:, u, :], window.indirect(entries(offs_sb, *span)))
+        for g in range(groups):
+            nc.scalar.copy(
+                woven[g][:].bitcast(U32).rearrange("p (s u) -> p s u", u=2),
+                halves[g][:].rearrange("p u s -> p s u"),
+            )
+        for g, (s0, s1) in enumerate(spans):
+            quantise(1, woven[g], s0, s1)
+            multiply(banks[g], 1, 0, s0, s1)
+            nc.scalar.copy(y[0][:, s0:s1], banks[g][:])
+        multiply(wide_bank, 1, 1, 0, S)
+        nc.scalar.copy(y[1][:], wide_bank[:])
 
         won = [keep.tile([P, V], F32, name="won%d" % b) for b in range(N // P)]
         lost = [keep.tile([P, V], F32, name="lost%d" % b) for b in range(N // P)]
@@ -137,7 +141,7 @@ def tile_picked_ranknet_sigmoid_e_kernel(tc, xT, w1_words, w1_scales, offs, win,
         result = [keep.tile([P, V], F32, name="result%d" % b) for b in range(N // P)]
 
         def fetch(dst, b, places, v0, v1):
-            nc.vector.tensor_copy(dst[b][:, v0:v1], y[b][:].indirect(places[:, v0 // LIST_ROWS : v1 // LIST_ROWS]))
+            nc.vector.tensor_copy(dst[b][:, v0:v1], y[b][:].indirect(entries(places, v0, v1)))
 
         def compare(b, v0, v1):
             nc.vector.tensor_tensor(margin[b][:, v0:v1], won[b][:, v0:v1], lost[b][:, v0:v1], SUBTRACT)
@@ -152,5 +156,6 @@ def tile_picked_ranknet_sigmoid_e_kernel(tc, xT, w1_words, w1_scales, offs, win,
         fetch(lost, 1, lose_sb, 0, half)
         fetch(lost, 1, lose_sb, half, V)
         compare(1, 0, half)
+        nc.sync.dma_start(out=out[P : 2 * P, :half], in_=result[1][:, :half])
         compare(1, half, V)
-        nc.sync.dma_start(out=out[P : 2 * P, :], in_=result[1][:])
+        nc.sync.dma_start(out=out[P : 2 * P, half:], in_=result[1][:, half:])

@@ -54,7 +54,7 @@ def tile_picked_ranknet_sigmoid_e_kernel(tc, xT, w1_words, w1_scales, offs, win,
                 in_=w1_scales[:, 4 * q : 4 * q + 4, :].rearrange("z r n -> r z n").bitcast(I32),
             )
 
-        w_words = [keep.tile([P, 2 * N], U8, name="w_words%d" % z, align_bytes=64) for z in range(PASSES)]
+        w_words = keep.tile([P, PASSES, 2 * N], U8, name="w_words", align_bytes=64)
 
         raw = {}
         for pair in range(2 * PASSES):
@@ -64,9 +64,7 @@ def tile_picked_ranknet_sigmoid_e_kernel(tc, xT, w1_words, w1_scales, offs, win,
                 nc.sync.dma_start(out=raw[pair, c0][:], in_=x_rows[z, :, 2 * u : 2 * u + 2, c0:c1])
                 if (pair, c0) == (0, 0):
                     nc.sync.dma_start(offs_sb[:], offs)
-            if pair == 1:
-                nc.sync.dma_start(out=w_words[0][:], in_=w1_words[0])
-        nc.sync.dma_start(out=w_words[1][:], in_=w1_words[1])
+        nc.sync.dma_start(out=w_words[:], in_=w1_words.rearrange("z p n -> p z n"))
         nc.sync.dma_start(win_sb[:], win)
         nc.sync.dma_start(lose_sb[:], lose)
 
@@ -98,7 +96,7 @@ def tile_picked_ranknet_sigmoid_e_kernel(tc, xT, w1_words, w1_scales, offs, win,
         def multiply(bank, z, b, s0, s1):
             nc.tensor.matmul_mx(
                 out=bank[:],
-                lhsT=w_words[z][:, 2 * P * b : 2 * P * (b + 1)].bitcast(FP4X4),
+                lhsT=w_words[:, z, 2 * P * b : 2 * P * (b + 1)].bitcast(FP4X4),
                 lhsT_scale=w_scales[:, z, P * b : P * (b + 1)],
                 rhs=codes[z][:, s0:s1].bitcast(FP8X4),
                 rhs_scale=scales[z][:, s0:s1],
@@ -143,19 +141,19 @@ def tile_picked_ranknet_sigmoid_e_kernel(tc, xT, w1_words, w1_scales, offs, win,
         def fetch(dst, b, places, v0, v1):
             nc.vector.tensor_copy(dst[b][:, v0:v1], y[b][:].indirect(entries(places, v0, v1)))
 
-        def compare(b, v0, v1):
-            nc.vector.tensor_tensor(margin[b][:, v0:v1], won[b][:, v0:v1], lost[b][:, v0:v1], SUBTRACT)
+        def compare(engine, b, v0, v1):
+            engine.tensor_tensor(margin[b][:, v0:v1], won[b][:, v0:v1], lost[b][:, v0:v1], SUBTRACT)
             nc.scalar.activation(result[b][:, v0:v1], margin[b][:, v0:v1], SIGMOID)
 
         half = V // 2
         fetch(won, 0, win_sb, 0, V)
         fetch(lost, 0, lose_sb, 0, V)
         fetch(won, 1, win_sb, 0, V)
-        compare(0, 0, V)
+        compare(nc.gpsimd, 0, 0, V)
         nc.sync.dma_start(out=out[0:P, :], in_=result[0][:])
         fetch(lost, 1, lose_sb, 0, half)
         fetch(lost, 1, lose_sb, half, V)
-        compare(1, 0, half)
+        compare(nc.vector, 1, 0, half)
         nc.sync.dma_start(out=out[P : 2 * P, :half], in_=result[1][:, :half])
-        compare(1, half, V)
+        compare(nc.vector, 1, half, V)
         nc.sync.dma_start(out=out[P : 2 * P, half:], in_=result[1][:, half:])

@@ -23,7 +23,7 @@ LIST_ROWS = 16
 
 LOADS = [
     [(0, 1024, 656)],
-    [(0, 1024, 512)],
+    [(0, 1024, 672)],
     [(0, 512, 0), (512, 1024, 0)],
     [(0, 512, 0), (512, 1024, 256)],
 ]
@@ -48,11 +48,6 @@ def tile_picked_ranknet_sigmoid_e_kernel(tc, xT, w1_words, w1_scales, offs, win,
 
         w_scales = keep.tile([P, PASSES, N], U8, name="w_scales", align_bytes=64)
         nc.gpsimd.memset(w_scales[:].rearrange("p z n -> p (z n)").bitcast(I32), 0)
-        for q in range(4):
-            nc.gpsimd.dma_start(
-                out=w_scales[32 * q : 32 * q + 4].bitcast(I32),
-                in_=w1_scales[:, 4 * q : 4 * q + 4, :].rearrange("z r n -> r z n").bitcast(I32),
-            )
 
         w_words = keep.tile([P, PASSES, 2 * N], U8, name="w_words", align_bytes=64)
 
@@ -65,6 +60,11 @@ def tile_picked_ranknet_sigmoid_e_kernel(tc, xT, w1_words, w1_scales, offs, win,
                 if (pair, c0) == (0, 0):
                     nc.sync.dma_start(offs_sb[:], offs)
         nc.sync.dma_start(out=w_words[:], in_=w1_words.rearrange("z p n -> p z n"))
+        for q in range(4):
+            nc.sync.dma_start(
+                out=w_scales[32 * q : 32 * q + 4].bitcast(I32),
+                in_=w1_scales[:, 4 * q : 4 * q + 4, :].rearrange("z r n -> r z n").bitcast(I32),
+            )
         nc.sync.dma_start(win_sb[:], win)
         nc.sync.dma_start(lose_sb[:], lose)
 
@@ -106,11 +106,20 @@ def tile_picked_ranknet_sigmoid_e_kernel(tc, xT, w1_words, w1_scales, offs, win,
 
         spans = [(GROUP * g, GROUP * (g + 1)) for g in range(groups)]
 
-        picked = keep.tile([P, 4 * S], BF16, name="picked_first", align_bytes=64)
-        picked_words = picked[:].bitcast(U32).rearrange("p (s u) -> p s u", u=2)
+        parts = [(0, S // 2), (S // 2, S)]
+        first = [keep.tile([P, 2, S // 2], U32, name="first%d" % i) for i in range(2)]
+        first_woven = [keep.tile([P, 2 * S], BF16, name="first_woven%d" % i, align_bytes=64) for i in range(2)]
         for u in range(2):
-            nc.vector.tensor_copy(picked_words[:, :, u], cast(u).indirect(offs_sb[:]))
-        quantise(0, picked, 0, S)
+            window = cast(u)
+            for i, part in enumerate(parts):
+                nc.vector.tensor_copy(first[i][:, u, :], window.indirect(entries(offs_sb, *part)))
+        for i in range(2):
+            nc.vector.tensor_copy(
+                first_woven[i][:].bitcast(I32).rearrange("p (s u) -> p s u", u=2),
+                first[i][:].bitcast(I32).rearrange("p u s -> p s u"),
+            )
+        for i, part in enumerate(parts):
+            quantise(0, first_woven[i], *part)
         for g, span in enumerate(spans):
             multiply(banks[g], 0, 0, *span)
         multiply(wide_bank, 0, 1, 0, S)

@@ -17,21 +17,24 @@ SIGMOID = mybir.ActivationFunctionType.Sigmoid
 SUBTRACT = mybir.AluOpType.subtract
 
 P = 128
-PASSES = K // 512
-GROUP = 128
+PACK = 4
+PASSES = K // (P * PACK)
+QUADRANT = 32
+SCALE_ROWS = 4
 LIST_ROWS = 16
+GROUP = 128
 
 LOADS = [
     [(0, 1024, 656)],
     [(0, 1024, 672)],
     [(0, 512, 0), (512, 1024, 0)],
-    [(0, 512, 0), (512, 1024, 256)],
+    [(0, 512, 0), (512, 896, 256), (896, 1024, 0)],
 ]
 
 
 def tile_picked_ranknet_sigmoid_e_kernel(tc, xT, w1_words, w1_scales, offs, win, lose, out):
     nc = tc.nc
-    x_rows = xT.rearrange("(z p j) t -> z p j t", p=P, j=4)
+    x_rows = xT.rearrange("(z p j) t -> z p j t", p=P, j=PACK)
 
     with ExitStack() as ctx:
         keep = ctx.enter_context(tc.tile_pool(name="keep", bufs=1))
@@ -41,14 +44,8 @@ def tile_picked_ranknet_sigmoid_e_kernel(tc, xT, w1_words, w1_scales, offs, win,
         win_sb = keep.tile([P, V // LIST_ROWS], U16, name="win_sb")
         lose_sb = keep.tile([P, V // LIST_ROWS], U16, name="lose_sb")
 
-        warm_in = keep.tile([P, 8], F32, name="warm_in")
-        warm_out = keep.tile([P, 8], F32, name="warm_out")
-        nc.vector.memset(warm_in[:], 0.0)
-        nc.scalar.activation(warm_out[:], warm_in[:], SIGMOID)
-
         w_scales = keep.tile([P, PASSES, N], U8, name="w_scales", align_bytes=64)
         nc.gpsimd.memset(w_scales[:].rearrange("p z n -> p (z n)").bitcast(I32), 0)
-
         w_words = keep.tile([P, PASSES, 2 * N], U8, name="w_words", align_bytes=64)
 
         raw = {}
@@ -57,41 +54,40 @@ def tile_picked_ranknet_sigmoid_e_kernel(tc, xT, w1_words, w1_scales, offs, win,
             for c0, c1, by_vector in LOADS[pair]:
                 raw[pair, c0] = keep.tile([P, 2, c1 - c0], F32, name="raw%d_%d" % (pair, c0))
                 nc.sync.dma_start(out=raw[pair, c0][:], in_=x_rows[z, :, 2 * u : 2 * u + 2, c0:c1])
-                if (pair, c0) == (0, 0):
+                if len(raw) == 1:
                     nc.sync.dma_start(offs_sb[:], offs)
         nc.sync.dma_start(out=w_words[:], in_=w1_words.rearrange("z p n -> p z n"))
-        for q in range(4):
+        for q in range(P // QUADRANT):
             nc.sync.dma_start(
-                out=w_scales[32 * q : 32 * q + 4].bitcast(I32),
-                in_=w1_scales[:, 4 * q : 4 * q + 4, :].rearrange("z r n -> r z n").bitcast(I32),
+                out=w_scales[QUADRANT * q : QUADRANT * q + SCALE_ROWS].bitcast(I32),
+                in_=w1_scales[:, SCALE_ROWS * q : SCALE_ROWS * (q + 1), :].rearrange("z r n -> r z n").bitcast(I32),
             )
         nc.sync.dma_start(win_sb[:], win)
         nc.sync.dma_start(lose_sb[:], lose)
 
         groups = S // GROUP
-        banks = [psum.tile([P, GROUP], F32, name="bank%d" % g) for g in range(groups)]
+        group_banks = [psum.tile([P, GROUP], F32, name="group_bank%d" % g) for g in range(groups)]
         wide_bank = psum.tile([P, S], F32, name="wide_bank")
         y = [keep.tile([P, S], F32, name="y%d" % b) for b in range(N // P)]
         codes = [keep.tile([P, S], U32, name="codes%d" % z, align_bytes=64) for z in range(PASSES)]
         scales = [keep.tile([P, S], U8, name="scales%d" % z, align_bytes=64) for z in range(PASSES)]
 
-        def cast(pair):
+        def round_pair(pair):
             window = keep.tile([P, 2 * T], BF16, name="window%d" % pair, align_bytes=64)
             for c0, c1, by_vector in LOADS[pair]:
                 src = raw[pair, c0][:].rearrange("p e c -> p c e")
                 dst = window[:, 2 * c0 : 2 * c1].rearrange("p (c e) -> p c e", e=2)
                 by_scalar = c1 - c0 - by_vector
-                if by_scalar:
-                    nc.scalar.copy(dst[:, :by_scalar, :], src[:, :by_scalar, :])
+                nc.scalar.copy(dst[:, :by_scalar, :], src[:, :by_scalar, :])
                 if by_vector:
                     nc.vector.tensor_copy(dst[:, by_scalar:, :], src[:, by_scalar:, :])
             return window[:].bitcast(U32)
 
-        def entries(places, first, last):
-            return places[:, first // LIST_ROWS : last // LIST_ROWS]
+        def entries(places, first, end):
+            return places[:, first // LIST_ROWS : end // LIST_ROWS]
 
-        def quantise(z, picked, s0, s1):
-            nc.vector.quantize_mx(out=codes[z][:, s0:s1].bitcast(FP8X4), scales=scales[z][:, s0:s1], in_=picked[:])
+        def quantise(z, values, s0, s1):
+            nc.vector.quantize_mx(out=codes[z][:, s0:s1].bitcast(FP8X4), scales=scales[z][:, s0:s1], in_=values[:])
 
         def multiply(bank, z, b, s0, s1):
             nc.tensor.matmul_mx(
@@ -104,41 +100,43 @@ def tile_picked_ranknet_sigmoid_e_kernel(tc, xT, w1_words, w1_scales, offs, win,
                 stop=(z == PASSES - 1),
             )
 
-        spans = [(GROUP * g, GROUP * (g + 1)) for g in range(groups)]
+        group_spans = [(GROUP * g, GROUP * (g + 1)) for g in range(groups)]
 
-        parts = [(0, S // 2), (S // 2, S)]
-        first = [keep.tile([P, 2, S // 2], U32, name="first%d" % i) for i in range(2)]
-        first_woven = [keep.tile([P, 2 * S], BF16, name="first_woven%d" % i, align_bytes=64) for i in range(2)]
-        for u in range(2):
-            window = cast(u)
-            for i, part in enumerate(parts):
-                nc.vector.tensor_copy(first[i][:, u, :], window.indirect(entries(offs_sb, *part)))
+        half_spans = [(0, S // 2), (S // 2, S)]
+        picked0_tile = keep.tile([P, 2 * S], U32, name="picked0")
+        picked0 = picked0_tile[:].rearrange("p (i u s) -> p i u s", i=2, u=2)
+        woven0 = [keep.tile([P, PACK * S // 2], BF16, name="woven0_%d" % i, align_bytes=64) for i in range(2)]
+        nc.vector.tensor_copy(picked0[:, :, 0, :], round_pair(0).indirect(offs_sb[:]))
+        window1 = round_pair(1)
+        for i, span in enumerate(half_spans):
+            nc.vector.tensor_copy(picked0[:, i, 1, :], window1.indirect(entries(offs_sb, *span)))
         for i in range(2):
             nc.vector.tensor_copy(
-                first_woven[i][:].bitcast(I32).rearrange("p (s u) -> p s u", u=2),
-                first[i][:].bitcast(I32).rearrange("p u s -> p s u"),
+                woven0[i][:].bitcast(I32).rearrange("p (s u) -> p s u", u=2),
+                picked0[:, i].bitcast(I32).rearrange("p u s -> p s u"),
             )
-        for i, part in enumerate(parts):
-            quantise(0, first_woven[i], *part)
-        for g, span in enumerate(spans):
-            multiply(banks[g], 0, 0, *span)
+        for i, span in enumerate(half_spans):
+            quantise(0, woven0[i], *span)
+        for g, span in enumerate(group_spans):
+            multiply(group_banks[g], 0, 0, *span)
         multiply(wide_bank, 0, 1, 0, S)
 
-        halves = [keep.tile([P, 2, GROUP], U32, name="halves%d" % g) for g in range(groups)]
-        woven = [keep.tile([P, 4 * GROUP], BF16, name="woven%d" % g, align_bytes=64) for g in range(groups)]
-        for u in range(2):
-            window = cast(2 + u)
-            for g, span in enumerate(spans):
-                nc.vector.tensor_copy(halves[g][:, u, :], window.indirect(entries(offs_sb, *span)))
+        picked1_tile = keep.tile([P, 2 * S], U32, name="picked1")
+        picked1 = picked1_tile[:].rearrange("p (g u s) -> p g u s", u=2, s=GROUP)
+        woven1 = [keep.tile([P, PACK * GROUP], BF16, name="woven1_%d" % g, align_bytes=64) for g in range(groups)]
+        nc.vector.tensor_copy(picked1[:, :, 0, :], round_pair(2).indirect(offs_sb[:]))
+        window3 = round_pair(3)
+        for g, span in enumerate(group_spans):
+            nc.vector.tensor_copy(picked1[:, g, 1, :], window3.indirect(entries(offs_sb, *span)))
         for g in range(groups):
             nc.scalar.copy(
-                woven[g][:].bitcast(U32).rearrange("p (s u) -> p s u", u=2),
-                halves[g][:].rearrange("p u s -> p s u"),
+                woven1[g][:].bitcast(U32).rearrange("p (s u) -> p s u", u=2),
+                picked1[:, g].rearrange("p u s -> p s u"),
             )
-        for g, (s0, s1) in enumerate(spans):
-            quantise(1, woven[g], s0, s1)
-            multiply(banks[g], 1, 0, s0, s1)
-            nc.scalar.copy(y[0][:, s0:s1], banks[g][:])
+        for g, (s0, s1) in enumerate(group_spans):
+            quantise(1, woven1[g], s0, s1)
+            multiply(group_banks[g], 1, 0, s0, s1)
+            nc.scalar.copy(y[0][:, s0:s1], group_banks[g][:])
         multiply(wide_bank, 1, 1, 0, S)
         nc.scalar.copy(y[1][:], wide_bank[:])
 
@@ -153,16 +151,13 @@ def tile_picked_ranknet_sigmoid_e_kernel(tc, xT, w1_words, w1_scales, offs, win,
         def compare(engine, b, v0, v1):
             engine.tensor_tensor(margin[b][:, v0:v1], won[b][:, v0:v1], lost[b][:, v0:v1], SUBTRACT)
             nc.scalar.activation(result[b][:, v0:v1], margin[b][:, v0:v1], SIGMOID)
+            nc.sync.dma_start(out=out[P * b : P * (b + 1), v0:v1], in_=result[b][:, v0:v1])
 
-        half = V // 2
         fetch(won, 0, win_sb, 0, V)
         fetch(lost, 0, lose_sb, 0, V)
         fetch(won, 1, win_sb, 0, V)
         compare(nc.gpsimd, 0, 0, V)
-        nc.sync.dma_start(out=out[0:P, :], in_=result[0][:])
-        fetch(lost, 1, lose_sb, 0, half)
-        fetch(lost, 1, lose_sb, half, V)
-        compare(nc.vector, 1, 0, half)
-        nc.sync.dma_start(out=out[P : 2 * P, :half], in_=result[1][:, :half])
-        compare(nc.vector, 1, half, V)
-        nc.sync.dma_start(out=out[P : 2 * P, half:], in_=result[1][:, half:])
+        fetch(lost, 1, lose_sb, 0, V // 2)
+        fetch(lost, 1, lose_sb, V // 2, V)
+        compare(nc.vector, 1, 0, V // 2)
+        compare(nc.vector, 1, V // 2, V)

@@ -48,6 +48,10 @@ def tile_picked_ranknet_sigmoid_e_kernel(tc, xT, w1_words, w1_scales, offs, win,
         nc.gpsimd.memset(w_scales[:].rearrange("p z n -> p (z n)").bitcast(I32), 0)
         w_words = keep.tile([P, PASSES, 2 * N], U8, name="w_words", align_bytes=64)
 
+        warm = keep.tile([P, 2], F32, name="warm")
+        nc.gpsimd.memset(warm[:, 0:1], 0.0)
+        nc.scalar.activation(warm[:, 1:2], warm[:, 0:1], SIGMOID)
+
         raw = {}
         for pair in range(2 * PASSES):
             z, u = divmod(pair, 2)
@@ -140,24 +144,28 @@ def tile_picked_ranknet_sigmoid_e_kernel(tc, xT, w1_words, w1_scales, offs, win,
         multiply(wide_bank, 1, 1, 0, S)
         nc.scalar.copy(y[1][:], wide_bank[:])
 
-        won = [keep.tile([P, V], F32, name="won%d" % b) for b in range(N // P)]
         lost = [keep.tile([P, V], F32, name="lost%d" % b) for b in range(N // P)]
         margin = [keep.tile([P, V], F32, name="margin%d" % b) for b in range(N // P)]
         result = [keep.tile([P, V], F32, name="result%d" % b) for b in range(N // P)]
 
-        def fetch(dst, b, places, v0, v1):
-            nc.vector.tensor_copy(dst[b][:, v0:v1], y[b][:].indirect(entries(places, v0, v1)))
+        def fetch_losers(b, v0, v1):
+            nc.vector.tensor_copy(lost[b][:, v0:v1], y[b][:].indirect(entries(lose_sb, v0, v1)))
 
-        def compare(engine, b, v0, v1):
-            engine.tensor_tensor(margin[b][:, v0:v1], won[b][:, v0:v1], lost[b][:, v0:v1], SUBTRACT)
+        def subtract(b, v0, v1):
+            nc.vector.tensor_tensor(margin[b][:, v0:v1], y[b][:].indirect(entries(win_sb, v0, v1)), lost[b][:, v0:v1], SUBTRACT)
+
+        def finish(b, v0, v1):
             nc.scalar.activation(result[b][:, v0:v1], margin[b][:, v0:v1], SIGMOID)
             nc.sync.dma_start(out=out[P * b : P * (b + 1), v0:v1], in_=result[b][:, v0:v1])
 
-        fetch(won, 0, win_sb, 0, V)
-        fetch(lost, 0, lose_sb, 0, V)
-        fetch(won, 1, win_sb, 0, V)
-        compare(nc.gpsimd, 0, 0, V)
-        fetch(lost, 1, lose_sb, 0, V // 2)
-        fetch(lost, 1, lose_sb, V // 2, V)
-        compare(nc.vector, 1, 0, V // 2)
-        compare(nc.vector, 1, V // 2, V)
+        fetch_losers(0, 0, V // 2)
+        fetch_losers(0, V // 2, V)
+        subtract(0, 0, V // 2)
+        subtract(0, V // 2, V)
+        finish(0, 0, V)
+        fetch_losers(1, 0, V // 2)
+        fetch_losers(1, V // 2, V)
+        subtract(1, 0, V // 2)
+        finish(1, 0, V // 2)
+        subtract(1, V // 2, V)
+        finish(1, V // 2, V)

@@ -25,11 +25,12 @@ LIST_ROWS = 16
 GROUP = 128
 
 LOADS = [
-    [(0, 1024, 656)],
     [(0, 1024, 672)],
-    [(0, 512, 0), (512, 1024, 0)],
-    [(0, 512, 0), (512, 896, 256), (896, 1024, 0)],
+    [(0, 1024, 672)],
+    [(0, 1024, 1024)],
+    [(0, 512, 0), (512, 1024, 336)],
 ]
+HELD = 32
 
 
 def tile_picked_ranknet_sigmoid_e_kernel(tc, xT, w1_words, w1_scales, offs, win, lose, out):
@@ -52,12 +53,19 @@ def tile_picked_ranknet_sigmoid_e_kernel(tc, xT, w1_words, w1_scales, offs, win,
         nc.gpsimd.memset(warm[:, 0:1], 0.0)
         nc.scalar.activation(warm[:, 1:2], warm[:, 0:1], SIGMOID)
 
+        shared = [
+            keep.tile([P, S - 2 * HELD + 2 * LOADS[2 + i][0][1]], F32, name="shared%d" % i, align_bytes=64)
+            for i in range(2)
+        ]
         raw = {}
         for pair in range(2 * PASSES):
             z, u = divmod(pair, 2)
             for c0, c1, by_vector in LOADS[pair]:
-                raw[pair, c0] = keep.tile([P, 2, c1 - c0], F32, name="raw%d_%d" % (pair, c0))
-                nc.sync.dma_start(out=raw[pair, c0][:], in_=x_rows[z, :, 2 * u : 2 * u + 2, c0:c1])
+                if pair >= 2 and c0 == 0:
+                    raw[pair, c0] = shared[pair - 2][:, S - 2 * HELD :].rearrange("p (e c) -> p e c", e=2)
+                else:
+                    raw[pair, c0] = keep.tile([P, 2, c1 - c0], F32, name="raw%d_%d" % (pair, c0))[:]
+                nc.sync.dma_start(out=raw[pair, c0], in_=x_rows[z, :, 2 * u : 2 * u + 2, c0:c1])
                 if len(raw) == 1:
                     nc.sync.dma_start(offs_sb[:], offs)
         nc.sync.dma_start(out=w_words[:], in_=w1_words.rearrange("z p n -> p z n"))
@@ -76,14 +84,24 @@ def tile_picked_ranknet_sigmoid_e_kernel(tc, xT, w1_words, w1_scales, offs, win,
         codes = [keep.tile([P, S], U32, name="codes%d" % z, align_bytes=64) for z in range(PASSES)]
         scales = [keep.tile([P, S], U8, name="scales%d" % z, align_bytes=64) for z in range(PASSES)]
 
-        def round_pair(pair):
+        def round_pair(pair, after_first_piece=None):
             window = keep.tile([P, 2 * T], BF16, name="window%d" % pair, align_bytes=64)
             for c0, c1, by_vector in LOADS[pair]:
-                src = raw[pair, c0][:].rearrange("p e c -> p c e")
+                src = raw[pair, c0].rearrange("p e c -> p c e")
                 dst = window[:, 2 * c0 : 2 * c1].rearrange("p (c e) -> p c e", e=2)
                 by_scalar = c1 - c0 - by_vector
-                nc.scalar.copy(dst[:, :by_scalar, :], src[:, :by_scalar, :])
-                if by_vector:
+                if by_vector == 0:
+                    nc.scalar.copy(dst[:, : by_scalar // 2, :], src[:, : by_scalar // 2, :])
+                    nc.scalar.copy(dst[:, by_scalar // 2 :, :], src[:, by_scalar // 2 :, :])
+                    after_first_piece()
+                elif by_scalar:
+                    nc.scalar.copy(dst[:, :by_scalar, :], src[:, :by_scalar, :])
+                if by_scalar == 0:
+                    nc.vector.tensor_copy(dst[:, :256, :], src[:, :256, :])
+                    nc.vector.tensor_copy(dst[:, 256:640, :], src[:, 256:640, :])
+                    after_first_piece()
+                    nc.vector.tensor_copy(dst[:, 640:, :], src[:, 640:, :])
+                elif by_vector:
                     nc.vector.tensor_copy(dst[:, by_scalar:, :], src[:, by_scalar:, :])
             return window[:].bitcast(U32)
 
@@ -91,7 +109,7 @@ def tile_picked_ranknet_sigmoid_e_kernel(tc, xT, w1_words, w1_scales, offs, win,
             return places[:, first // LIST_ROWS : end // LIST_ROWS]
 
         def quantise(z, values, s0, s1):
-            nc.vector.quantize_mx(out=codes[z][:, s0:s1].bitcast(FP8X4), scales=scales[z][:, s0:s1], in_=values[:])
+            nc.vector.quantize_mx(out=codes[z][:, s0:s1].bitcast(FP8X4), scales=scales[z][:, s0:s1], in_=values)
 
         def multiply(bank, z, b, s0, s1):
             nc.tensor.matmul_mx(
@@ -107,38 +125,43 @@ def tile_picked_ranknet_sigmoid_e_kernel(tc, xT, w1_words, w1_scales, offs, win,
         group_spans = [(GROUP * g, GROUP * (g + 1)) for g in range(groups)]
 
         half_spans = [(0, S // 2), (S // 2, S)]
+
+        def weave(woven, picked):
+            nc.scalar.copy(woven.bitcast(U32).rearrange("p (s u) -> p s u", u=2), picked.rearrange("p u s -> p s u"))
+
         picked0_tile = keep.tile([P, 2 * S], U32, name="picked0")
         picked0 = picked0_tile[:].rearrange("p (i u s) -> p i u s", i=2, u=2)
-        woven0 = [keep.tile([P, PACK * S // 2], BF16, name="woven0_%d" % i, align_bytes=64) for i in range(2)]
         nc.vector.tensor_copy(picked0[:, :, 0, :], round_pair(0).indirect(offs_sb[:]))
-        window1 = round_pair(1)
-        for i, span in enumerate(half_spans):
-            nc.vector.tensor_copy(picked0[:, i, 1, :], window1.indirect(entries(offs_sb, *span)))
+        nc.vector.tensor_copy(picked0[:, :, 1, :], round_pair(1).indirect(offs_sb[:]))
+        early = S // 2 - HELD
         for i in range(2):
-            nc.vector.tensor_copy(
-                woven0[i][:].bitcast(I32).rearrange("p (s u) -> p s u", u=2),
-                picked0[:, i].bitcast(I32).rearrange("p u s -> p s u"),
-            )
-        for i, span in enumerate(half_spans):
-            quantise(0, woven0[i], *span)
-        for g, span in enumerate(group_spans):
-            multiply(group_banks[g], 0, 0, *span)
-        multiply(wide_bank, 0, 1, 0, S)
+            weave(shared[i][:, : 2 * early], picked0[:, i, :, :early])
+        window2 = round_pair(
+            2,
+            lambda: nc.vector.tensor_copy(
+                shared[0][:, 2 * early : S].bitcast(I32).rearrange("p (s u) -> p s u", u=2),
+                picked0[:, 0, :, early:].bitcast(I32).rearrange("p u s -> p s u"),
+            ),
+        )
+        quantise(0, shared[0][:, :S].bitcast(BF16), *half_spans[0])
+        for g in range(groups // 2):
+            multiply(group_banks[g], 0, 0, *group_spans[g])
 
         picked1_tile = keep.tile([P, 2 * S], U32, name="picked1")
         picked1 = picked1_tile[:].rearrange("p (g u s) -> p g u s", u=2, s=GROUP)
         woven1 = [keep.tile([P, PACK * GROUP], BF16, name="woven1_%d" % g, align_bytes=64) for g in range(groups)]
-        nc.vector.tensor_copy(picked1[:, :, 0, :], round_pair(2).indirect(offs_sb[:]))
-        window3 = round_pair(3)
+        nc.vector.tensor_copy(picked1[:, :, 0, :], window2.indirect(offs_sb[:]))
+        window3 = round_pair(3, lambda: weave(shared[1][:, 2 * early : S], picked0[:, 1, :, early:]))
+        quantise(0, shared[1][:, :S].bitcast(BF16), *half_spans[1])
+        for g in range(groups // 2, groups):
+            multiply(group_banks[g], 0, 0, *group_spans[g])
+        multiply(wide_bank, 0, 1, 0, S)
         for g, span in enumerate(group_spans):
             nc.vector.tensor_copy(picked1[:, g, 1, :], window3.indirect(entries(offs_sb, *span)))
         for g in range(groups):
-            nc.scalar.copy(
-                woven1[g][:].bitcast(U32).rearrange("p (s u) -> p s u", u=2),
-                picked1[:, g].rearrange("p u s -> p s u"),
-            )
+            weave(woven1[g][:], picked1[:, g])
         for g, (s0, s1) in enumerate(group_spans):
-            quantise(1, woven1[g], s0, s1)
+            quantise(1, woven1[g][:], s0, s1)
             multiply(group_banks[g], 1, 0, s0, s1)
             nc.scalar.copy(y[0][:, s0:s1], group_banks[g][:])
         multiply(wide_bank, 1, 1, 0, S)

@@ -24,12 +24,8 @@ SCALE_ROWS = 4
 LIST_ROWS = 16
 GROUP = 128
 
-LOADS = [
-    [(0, 1024, 672)],
-    [(0, 1024, 672)],
-    [(0, 1024, 1024)],
-    [(0, 512, 0), (512, 1024, 336)],
-]
+LOADS = [(0, 0, T), (1, 0, T), (2, 0, T), (3, 0, T // 2), (3, T // 2, T)]
+OVERLAP = 16
 HELD = 32
 
 
@@ -53,21 +49,23 @@ def tile_picked_ranknet_sigmoid_e_kernel(tc, xT, w1_words, w1_scales, offs, win,
         nc.gpsimd.memset(warm[:, 0:1], 0.0)
         nc.scalar.activation(warm[:, 1:2], warm[:, 0:1], SIGMOID)
 
-        shared = [
-            keep.tile([P, S - 2 * HELD + 2 * LOADS[2 + i][0][1]], F32, name="shared%d" % i, align_bytes=64)
-            for i in range(2)
-        ]
-        raw = {}
-        for pair in range(2 * PASSES):
+        half_words = S
+        raw2_at = half_words - 2 * HELD
+        second_at = raw2_at + 2 * T - OVERLAP
+        raw3_at = second_at + half_words - 2 * HELD
+        shared = keep.tile([P, raw3_at + T], F32, name="shared", align_bytes=64)
+        woven0 = [shared[:, :half_words], shared[:, second_at : second_at + half_words]]
+        raw = {
+            (2, 0): shared[:, raw2_at : raw2_at + 2 * T].rearrange("p (e c) -> p e c", e=2),
+            (3, 0): shared[:, raw3_at:].rearrange("p (e c) -> p e c", e=2),
+        }
+        for pair, c0, c1 in LOADS:
             z, u = divmod(pair, 2)
-            for c0, c1, by_vector in LOADS[pair]:
-                if pair >= 2 and c0 == 0:
-                    raw[pair, c0] = shared[pair - 2][:, S - 2 * HELD :].rearrange("p (e c) -> p e c", e=2)
-                else:
-                    raw[pair, c0] = keep.tile([P, 2, c1 - c0], F32, name="raw%d_%d" % (pair, c0))[:]
-                nc.sync.dma_start(out=raw[pair, c0], in_=x_rows[z, :, 2 * u : 2 * u + 2, c0:c1])
-                if len(raw) == 1:
-                    nc.sync.dma_start(offs_sb[:], offs)
+            if (pair, c0) not in raw:
+                raw[pair, c0] = keep.tile([P, 2, c1 - c0], F32, name="raw%d_%d" % (pair, c0))[:]
+            nc.sync.dma_start(out=raw[pair, c0], in_=x_rows[z, :, 2 * u : 2 * u + 2, c0:c1])
+            if pair == 0:
+                nc.sync.dma_start(offs_sb[:], offs)
         nc.sync.dma_start(out=w_words[:], in_=w1_words.rearrange("z p n -> p z n"))
         for q in range(P // QUADRANT):
             nc.sync.dma_start(
@@ -84,26 +82,13 @@ def tile_picked_ranknet_sigmoid_e_kernel(tc, xT, w1_words, w1_scales, offs, win,
         codes = [keep.tile([P, S], U32, name="codes%d" % z, align_bytes=64) for z in range(PASSES)]
         scales = [keep.tile([P, S], U8, name="scales%d" % z, align_bytes=64) for z in range(PASSES)]
 
-        def round_pair(pair, after_first_piece=None):
-            window = keep.tile([P, 2 * T], BF16, name="window%d" % pair, align_bytes=64)
-            for c0, c1, by_vector in LOADS[pair]:
-                src = raw[pair, c0].rearrange("p e c -> p c e")
-                dst = window[:, 2 * c0 : 2 * c1].rearrange("p (c e) -> p c e", e=2)
-                by_scalar = c1 - c0 - by_vector
-                if by_vector == 0:
-                    nc.scalar.copy(dst[:, : by_scalar // 2, :], src[:, : by_scalar // 2, :])
-                    nc.scalar.copy(dst[:, by_scalar // 2 :, :], src[:, by_scalar // 2 :, :])
-                    after_first_piece()
-                elif by_scalar:
-                    nc.scalar.copy(dst[:, :by_scalar, :], src[:, :by_scalar, :])
-                if by_scalar == 0:
-                    nc.vector.tensor_copy(dst[:, :256, :], src[:, :256, :])
-                    nc.vector.tensor_copy(dst[:, 256:640, :], src[:, 256:640, :])
-                    after_first_piece()
-                    nc.vector.tensor_copy(dst[:, 640:, :], src[:, 640:, :])
-                elif by_vector:
-                    nc.vector.tensor_copy(dst[:, by_scalar:, :], src[:, by_scalar:, :])
-            return window[:].bitcast(U32)
+        windows = [keep.tile([P, 2 * T], BF16, name="window%d" % pair, align_bytes=64) for pair in range(2 * PASSES)]
+
+        def round_docs(copy, pair, piece, c0, c1):
+            copy(
+                windows[pair][:, 2 * c0 : 2 * c1].rearrange("p (c e) -> p c e", e=2),
+                raw[pair, piece][:, :, c0 - piece : c1 - piece].rearrange("p e c -> p c e"),
+            )
 
         def entries(places, first, end):
             return places[:, first // LIST_ROWS : end // LIST_ROWS]
@@ -126,42 +111,62 @@ def tile_picked_ranknet_sigmoid_e_kernel(tc, xT, w1_words, w1_scales, offs, win,
 
         half_spans = [(0, S // 2), (S // 2, S)]
 
-        def weave(woven, picked):
-            nc.scalar.copy(woven.bitcast(U32).rearrange("p (s u) -> p s u", u=2), picked.rearrange("p u s -> p s u"))
+        on_scalar, on_vector = nc.scalar.copy, nc.vector.tensor_copy
+
+        def weave(copy, woven, picked):
+            copy(woven.bitcast(U32).rearrange("p (s u) -> p s u", u=2), picked.rearrange("p u s -> p s u"))
+
+        def weave_on_vector(woven, picked):
+            on_vector(woven.bitcast(I32).rearrange("p (s u) -> p s u", u=2), picked.bitcast(I32).rearrange("p u s -> p s u"))
+
+        def gather(dst, pair, s0, s1):
+            nc.vector.tensor_copy(dst, windows[pair][:].bitcast(U32).indirect(entries(offs_sb, s0, s1)))
 
         picked0_tile = keep.tile([P, 2 * S], U32, name="picked0")
         picked0 = picked0_tile[:].rearrange("p (i u s) -> p i u s", i=2, u=2)
-        nc.vector.tensor_copy(picked0[:, :, 0, :], round_pair(0).indirect(offs_sb[:]))
-        nc.vector.tensor_copy(picked0[:, :, 1, :], round_pair(1).indirect(offs_sb[:]))
+        round_docs(on_scalar, 0, 0, 0, 352)
+        round_docs(on_vector, 0, 0, 352, T)
+        gather(picked0[:, :, 0, :], 0, 0, S)
+        round_docs(on_scalar, 1, 0, 0, 352)
+        round_docs(on_vector, 1, 0, 352, T)
+        for i, span in enumerate(half_spans):
+            gather(picked0[:, i, 1, :], 1, *span)
         early = S // 2 - HELD
-        for i in range(2):
-            weave(shared[i][:, : 2 * early], picked0[:, i, :, :early])
-        window2 = round_pair(
-            2,
-            lambda: nc.vector.tensor_copy(
-                shared[0][:, 2 * early : S].bitcast(I32).rearrange("p (s u) -> p s u", u=2),
-                picked0[:, 0, :, early:].bitcast(I32).rearrange("p u s -> p s u"),
-            ),
-        )
-        quantise(0, shared[0][:, :S].bitcast(BF16), *half_spans[0])
+        weave(on_scalar, woven0[0][:, : 2 * early], picked0[:, 0, :, :early])
+        round_docs(on_vector, 2, 0, 0, 64)
+        round_docs(on_vector, 2, 0, 768, T)
+        round_docs(on_scalar, 2, 0, 480, 768)
+        weave_on_vector(woven0[0][:, 2 * early :], picked0[:, 0, :, early:])
+        round_docs(on_vector, 2, 0, 64, 480)
+        weave(on_scalar, woven0[1][:, : 2 * early], picked0[:, 1, :, :early])
+        quantise(0, woven0[0].bitcast(BF16), *half_spans[0])
         for g in range(groups // 2):
             multiply(group_banks[g], 0, 0, *group_spans[g])
 
-        picked1_tile = keep.tile([P, 2 * S], U32, name="picked1")
+        picked1_tile = keep.tile([P, 2 * S], U32, name="picked1", align_bytes=64)
         picked1 = picked1_tile[:].rearrange("p (g u s) -> p g u s", u=2, s=GROUP)
-        woven1 = [keep.tile([P, PACK * GROUP], BF16, name="woven1_%d" % g, align_bytes=64) for g in range(groups)]
-        nc.vector.tensor_copy(picked1[:, :, 0, :], window2.indirect(offs_sb[:]))
-        window3 = round_pair(3, lambda: weave(shared[1][:, 2 * early : S], picked0[:, 1, :, early:]))
-        quantise(0, shared[1][:, :S].bitcast(BF16), *half_spans[1])
+        woven1 = [keep.tile([P, PACK * GROUP], BF16, name="woven1_%d" % g, align_bytes=64)[:] for g in range(groups - 1)]
+        woven1.append(picked1_tile[:, 2 * GROUP : 4 * GROUP].bitcast(BF16))
+        gather(picked1[:, :, 0, :], 2, 0, S)
+        round_docs(on_scalar, 3, 0, 0, 256)
+        round_docs(on_scalar, 3, 0, 256, 512)
+        weave(on_scalar, woven0[1][:, 2 * early :], picked0[:, 1, :, early:])
+        round_docs(on_scalar, 3, 512, 512, 688)
+        round_docs(on_vector, 3, 512, 688, T)
+        quantise(0, woven0[1].bitcast(BF16), *half_spans[1])
         for g in range(groups // 2, groups):
             multiply(group_banks[g], 0, 0, *group_spans[g])
         multiply(wide_bank, 0, 1, 0, S)
         for g, span in enumerate(group_spans):
-            nc.vector.tensor_copy(picked1[:, g, 1, :], window3.indirect(entries(offs_sb, *span)))
-        for g in range(groups):
-            weave(woven1[g][:], picked1[:, g])
+            gather(picked1[:, g, 1, :], 3, *span)
+        last = groups - 1
+        for g in range(last):
+            weave(on_scalar, woven1[g], picked1[:, g])
+        weave(on_scalar, woven1[last][:, : 2 * GROUP], picked1[:, last, :, : GROUP // 2])
         for g, (s0, s1) in enumerate(group_spans):
-            quantise(1, woven1[g][:], s0, s1)
+            if g == last - 1:
+                weave_on_vector(woven1[last][:, 2 * GROUP :], picked1[:, last, :, GROUP // 2 :])
+            quantise(1, woven1[g], s0, s1)
             multiply(group_banks[g], 1, 0, s0, s1)
             nc.scalar.copy(y[0][:, s0:s1], group_banks[g][:])
         multiply(wide_bank, 1, 1, 0, S)

@@ -19,14 +19,22 @@ SUBTRACT = mybir.AluOpType.subtract
 P = 128
 PACK = 4
 PASSES = K // (P * PACK)
+BLOCKS = N // P
 QUADRANT = 32
 SCALE_ROWS = 4
 LIST_ROWS = 16
 GROUP = 128
+GROUPS = S // GROUP
+HALF = S // 2
 
 LOADS = [(0, 0, T), (1, 0, T), (2, 0, T), (3, 0, T // 2), (3, T // 2, T)]
+
+SCALAR_OF_PAIR = 352
+SCALAR_OF_LAST = 176
+SCALAR_OF_PAIR2 = (480, 768)
+
+LATE = 32
 OVERLAP = 16
-HELD = 32
 
 
 def tile_picked_ranknet_sigmoid_e_kernel(tc, xT, w1_words, w1_scales, offs, win, lose, out):
@@ -42,59 +50,72 @@ def tile_picked_ranknet_sigmoid_e_kernel(tc, xT, w1_words, w1_scales, offs, win,
         lose_sb = keep.tile([P, V // LIST_ROWS], U16, name="lose_sb")
 
         w_scales = keep.tile([P, PASSES, N], U8, name="w_scales", align_bytes=64)
-        nc.gpsimd.memset(w_scales[:].rearrange("p z n -> p (z n)").bitcast(I32), 0)
+        w_scales_flat = w_scales[:].rearrange("p z n -> p (z n)")
+        nc.vector.memset(w_scales_flat.bitcast(I32), 0)
         w_words = keep.tile([P, PASSES, 2 * N], U8, name="w_words", align_bytes=64)
 
-        warm = keep.tile([P, 2], F32, name="warm")
-        nc.gpsimd.memset(warm[:, 0:1], 0.0)
-        nc.scalar.activation(warm[:, 1:2], warm[:, 0:1], SIGMOID)
+        warm_up = keep.tile([P, 1], F32, name="warm_up")
+        nc.scalar.activation(warm_up[:], w_scales_flat.bitcast(F32)[:, 0:1], SIGMOID)
 
-        half_words = S
-        raw2_at = half_words - 2 * HELD
-        second_at = raw2_at + 2 * T - OVERLAP
-        raw3_at = second_at + half_words - 2 * HELD
-        shared = keep.tile([P, raw3_at + T], F32, name="shared", align_bytes=64)
-        woven0 = [shared[:, :half_words], shared[:, second_at : second_at + half_words]]
-        raw = {
-            (2, 0): shared[:, raw2_at : raw2_at + 2 * T].rearrange("p (e c) -> p e c", e=2),
-            (3, 0): shared[:, raw3_at:].rearrange("p (e c) -> p e c", e=2),
+        woven_words = 2 * HALF
+        early = HALF - LATE
+        pair2_at = 2 * early
+        second_half_at = pair2_at + 2 * T - OVERLAP
+        pair3_at = second_half_at + 2 * early
+        shared = keep.tile([P, pair3_at + T], F32, name="shared", align_bytes=64)
+        woven0 = [shared[:, :woven_words], shared[:, second_half_at : second_half_at + woven_words]]
+        rows = {
+            (2, 0): shared[:, pair2_at : pair2_at + 2 * T].rearrange("p (e c) -> p e c", e=2),
+            (3, 0): shared[:, pair3_at:].rearrange("p (e c) -> p e c", e=2),
         }
+
         for pair, c0, c1 in LOADS:
             z, u = divmod(pair, 2)
-            if (pair, c0) not in raw:
-                raw[pair, c0] = keep.tile([P, 2, c1 - c0], F32, name="raw%d_%d" % (pair, c0))[:]
-            nc.sync.dma_start(out=raw[pair, c0], in_=x_rows[z, :, 2 * u : 2 * u + 2, c0:c1])
+            if (pair, c0) not in rows:
+                rows[pair, c0] = keep.tile([P, 2, c1 - c0], F32, name="rows%d_%d" % (pair, c0))[:]
+            nc.sync.dma_start(out=rows[pair, c0], in_=x_rows[z, :, 2 * u : 2 * u + 2, c0:c1])
             if pair == 0:
                 nc.sync.dma_start(offs_sb[:], offs)
-        nc.sync.dma_start(out=w_words[:], in_=w1_words.rearrange("z p n -> p z n"))
         for q in range(P // QUADRANT):
             nc.sync.dma_start(
                 out=w_scales[QUADRANT * q : QUADRANT * q + SCALE_ROWS].bitcast(I32),
                 in_=w1_scales[:, SCALE_ROWS * q : SCALE_ROWS * (q + 1), :].rearrange("z r n -> r z n").bitcast(I32),
             )
+        nc.sync.dma_start(out=w_words[:], in_=w1_words.rearrange("z p n -> p z n"))
         nc.sync.dma_start(win_sb[:], win)
         nc.sync.dma_start(lose_sb[:], lose)
 
-        groups = S // GROUP
-        group_banks = [psum.tile([P, GROUP], F32, name="group_bank%d" % g) for g in range(groups)]
+        group_banks = [psum.tile([P, GROUP], F32, name="group_bank%d" % g) for g in range(GROUPS)]
         wide_bank = psum.tile([P, S], F32, name="wide_bank")
-        y = [keep.tile([P, S], F32, name="y%d" % b) for b in range(N // P)]
+        y = [keep.tile([P, S], F32, name="y%d" % b) for b in range(BLOCKS)]
         codes = [keep.tile([P, S], U32, name="codes%d" % z, align_bytes=64) for z in range(PASSES)]
         scales = [keep.tile([P, S], U8, name="scales%d" % z, align_bytes=64) for z in range(PASSES)]
-
         windows = [keep.tile([P, 2 * T], BF16, name="window%d" % pair, align_bytes=64) for pair in range(2 * PASSES)]
 
-        def round_docs(copy, pair, piece, c0, c1):
+        group_spans = [(GROUP * g, GROUP * (g + 1)) for g in range(GROUPS)]
+        half_spans = [(0, HALF), (HALF, S)]
+        on_scalar, on_vector = nc.scalar.copy, nc.vector.tensor_copy
+
+        def round_docs(copy, pair, load_first, c0, c1):
             copy(
                 windows[pair][:, 2 * c0 : 2 * c1].rearrange("p (c e) -> p c e", e=2),
-                raw[pair, piece][:, :, c0 - piece : c1 - piece].rearrange("p e c -> p c e"),
+                rows[pair, load_first][:, :, c0 - load_first : c1 - load_first].rearrange("p e c -> p c e"),
             )
 
         def entries(places, first, end):
             return places[:, first // LIST_ROWS : end // LIST_ROWS]
 
-        def quantise(z, values, s0, s1):
-            nc.vector.quantize_mx(out=codes[z][:, s0:s1].bitcast(FP8X4), scales=scales[z][:, s0:s1], in_=values)
+        def gather(dst, pair, s0, s1):
+            nc.vector.tensor_copy(dst, windows[pair][:].bitcast(U32).indirect(entries(offs_sb, s0, s1)))
+
+        def weave_on_scalar(woven, picked):
+            on_scalar(woven.bitcast(U32).rearrange("p (s u) -> p s u", u=2), picked.rearrange("p u s -> p s u"))
+
+        def weave_on_vector(woven, picked):
+            on_vector(woven.bitcast(I32).rearrange("p (s u) -> p s u", u=2), picked.bitcast(I32).rearrange("p u s -> p s u"))
+
+        def quantise(z, woven, s0, s1):
+            nc.vector.quantize_mx(out=codes[z][:, s0:s1].bitcast(FP8X4), scales=scales[z][:, s0:s1], in_=woven)
 
         def multiply(bank, z, b, s0, s1):
             nc.tensor.matmul_mx(
@@ -107,74 +128,62 @@ def tile_picked_ranknet_sigmoid_e_kernel(tc, xT, w1_words, w1_scales, offs, win,
                 stop=(z == PASSES - 1),
             )
 
-        group_spans = [(GROUP * g, GROUP * (g + 1)) for g in range(groups)]
-
-        half_spans = [(0, S // 2), (S // 2, S)]
-
-        on_scalar, on_vector = nc.scalar.copy, nc.vector.tensor_copy
-
-        def weave(copy, woven, picked):
-            copy(woven.bitcast(U32).rearrange("p (s u) -> p s u", u=2), picked.rearrange("p u s -> p s u"))
-
-        def weave_on_vector(woven, picked):
-            on_vector(woven.bitcast(I32).rearrange("p (s u) -> p s u", u=2), picked.bitcast(I32).rearrange("p u s -> p s u"))
-
-        def gather(dst, pair, s0, s1):
-            nc.vector.tensor_copy(dst, windows[pair][:].bitcast(U32).indirect(entries(offs_sb, s0, s1)))
-
         picked0_tile = keep.tile([P, 2 * S], U32, name="picked0")
         picked0 = picked0_tile[:].rearrange("p (i u s) -> p i u s", i=2, u=2)
-        round_docs(on_scalar, 0, 0, 0, 352)
-        round_docs(on_vector, 0, 0, 352, T)
+        round_docs(on_scalar, 0, 0, 0, SCALAR_OF_PAIR)
+        round_docs(on_vector, 0, 0, SCALAR_OF_PAIR, T)
         gather(picked0[:, :, 0, :], 0, 0, S)
-        round_docs(on_scalar, 1, 0, 0, 352)
-        round_docs(on_vector, 1, 0, 352, T)
+        round_docs(on_scalar, 1, 0, 0, SCALAR_OF_PAIR)
+        round_docs(on_vector, 1, 0, SCALAR_OF_PAIR, T)
         for i, span in enumerate(half_spans):
             gather(picked0[:, i, 1, :], 1, *span)
-        early = S // 2 - HELD
-        weave(on_scalar, woven0[0][:, : 2 * early], picked0[:, 0, :, :early])
-        round_docs(on_vector, 2, 0, 0, 64)
-        round_docs(on_vector, 2, 0, 768, T)
-        round_docs(on_scalar, 2, 0, 480, 768)
+        weave_on_scalar(woven0[0][:, : 2 * early], picked0[:, 0, :, :early])
+
+        round_docs(on_vector, 2, 0, 0, 2 * LATE)
+        round_docs(on_vector, 2, 0, SCALAR_OF_PAIR2[1], T)
+        round_docs(on_scalar, 2, 0, *SCALAR_OF_PAIR2)
         weave_on_vector(woven0[0][:, 2 * early :], picked0[:, 0, :, early:])
-        round_docs(on_vector, 2, 0, 64, 480)
-        weave(on_scalar, woven0[1][:, : 2 * early], picked0[:, 1, :, :early])
+        round_docs(on_vector, 2, 0, 2 * LATE, SCALAR_OF_PAIR2[0])
+        weave_on_scalar(woven0[1][:, : 2 * early], picked0[:, 1, :, :early])
         quantise(0, woven0[0].bitcast(BF16), *half_spans[0])
-        for g in range(groups // 2):
+        for g in range(GROUPS // 2):
             multiply(group_banks[g], 0, 0, *group_spans[g])
 
         picked1_tile = keep.tile([P, 2 * S], U32, name="picked1", align_bytes=64)
         picked1 = picked1_tile[:].rearrange("p (g u s) -> p g u s", u=2, s=GROUP)
-        woven1 = [keep.tile([P, PACK * GROUP], BF16, name="woven1_%d" % g, align_bytes=64)[:] for g in range(groups - 1)]
+        last = GROUPS - 1
+        woven1 = [keep.tile([P, PACK * GROUP], BF16, name="woven1_%d" % g, align_bytes=64)[:] for g in range(last)]
         woven1.append(picked1_tile[:, 2 * GROUP : 4 * GROUP].bitcast(BF16))
         gather(picked1[:, :, 0, :], 2, 0, S)
-        round_docs(on_scalar, 3, 0, 0, 256)
-        round_docs(on_scalar, 3, 0, 256, 512)
-        weave(on_scalar, woven0[1][:, 2 * early :], picked0[:, 1, :, early:])
-        round_docs(on_scalar, 3, 512, 512, 688)
-        round_docs(on_vector, 3, 512, 688, T)
+
+        round_docs(on_scalar, 3, 0, 0, T // 4)
+        round_docs(on_scalar, 3, 0, T // 4, T // 2)
+        weave_on_scalar(woven0[1][:, 2 * early :], picked0[:, 1, :, early:])
+        round_docs(on_scalar, 3, T // 2, T // 2, T // 2 + SCALAR_OF_LAST)
+        round_docs(on_vector, 3, T // 2, T // 2 + SCALAR_OF_LAST, T)
         quantise(0, woven0[1].bitcast(BF16), *half_spans[1])
-        for g in range(groups // 2, groups):
+        for g in range(GROUPS // 2, GROUPS):
             multiply(group_banks[g], 0, 0, *group_spans[g])
         multiply(wide_bank, 0, 1, 0, S)
+
         for g, span in enumerate(group_spans):
             gather(picked1[:, g, 1, :], 3, *span)
-        last = groups - 1
         for g in range(last):
-            weave(on_scalar, woven1[g], picked1[:, g])
-        weave(on_scalar, woven1[last][:, : 2 * GROUP], picked1[:, last, :, : GROUP // 2])
+            weave_on_scalar(woven1[g], picked1[:, g])
+        half_group = GROUP // 2
+        weave_on_scalar(woven1[last][:, : PACK * half_group], picked1[:, last, :, :half_group])
         for g, (s0, s1) in enumerate(group_spans):
             if g == last - 1:
-                weave_on_vector(woven1[last][:, 2 * GROUP :], picked1[:, last, :, GROUP // 2 :])
+                weave_on_vector(woven1[last][:, PACK * half_group :], picked1[:, last, :, half_group:])
             quantise(1, woven1[g], s0, s1)
             multiply(group_banks[g], 1, 0, s0, s1)
             nc.scalar.copy(y[0][:, s0:s1], group_banks[g][:])
         multiply(wide_bank, 1, 1, 0, S)
         nc.scalar.copy(y[1][:], wide_bank[:])
 
-        lost = [keep.tile([P, V], F32, name="lost%d" % b) for b in range(N // P)]
-        margin = [keep.tile([P, V], F32, name="margin%d" % b) for b in range(N // P)]
-        result = [keep.tile([P, V], F32, name="result%d" % b) for b in range(N // P)]
+        lost = [keep.tile([P, V], F32, name="lost%d" % b) for b in range(BLOCKS)]
+        margin = [keep.tile([P, V], F32, name="margin%d" % b) for b in range(BLOCKS)]
+        result = [keep.tile([P, V], F32, name="result%d" % b) for b in range(BLOCKS)]
 
         def fetch_losers(b, v0, v1):
             nc.vector.tensor_copy(lost[b][:, v0:v1], y[b][:].indirect(entries(lose_sb, v0, v1)))
@@ -186,14 +195,14 @@ def tile_picked_ranknet_sigmoid_e_kernel(tc, xT, w1_words, w1_scales, offs, win,
             nc.scalar.activation(result[b][:, v0:v1], margin[b][:, v0:v1], SIGMOID)
             nc.sync.dma_start(out=out[P * b : P * (b + 1), v0:v1], in_=result[b][:, v0:v1])
 
-        fetch_losers(0, 0, V // 2)
-        fetch_losers(0, V // 2, V)
-        subtract(0, 0, V // 2)
-        subtract(0, V // 2, V)
+        compared_halves = [(0, V // 2), (V // 2, V)]
+        for half in compared_halves:
+            fetch_losers(0, *half)
+        for half in compared_halves:
+            subtract(0, *half)
         finish(0, 0, V)
-        fetch_losers(1, 0, V // 2)
-        fetch_losers(1, V // 2, V)
-        subtract(1, 0, V // 2)
-        finish(1, 0, V // 2)
-        subtract(1, V // 2, V)
-        finish(1, V // 2, V)
+        for half in compared_halves:
+            fetch_losers(1, *half)
+        for half in compared_halves:
+            subtract(1, *half)
+            finish(1, *half)

@@ -31,7 +31,7 @@ LOADS = [(0, 0, T), (1, 0, T), (2, 0, T), (3, 0, T // 2), (3, T // 2, T)]
 
 SCALAR_OF_PAIR = 352
 SCALAR_OF_LAST = 176
-SCALAR_OF_PAIR2 = (480, 768)
+SCALAR_OF_PAIR2 = (416, 768)
 
 LATE = 32
 OVERLAP = 16
@@ -135,9 +135,11 @@ def tile_picked_ranknet_sigmoid_e_kernel(tc, xT, w1_words, w1_scales, offs, win,
         gather(picked0[:, :, 0, :], 0, 0, S)
         round_docs(on_scalar, 1, 0, 0, SCALAR_OF_PAIR)
         round_docs(on_vector, 1, 0, SCALAR_OF_PAIR, T)
-        for i, span in enumerate(half_spans):
-            gather(picked0[:, i, 1, :], 1, *span)
-        weave_on_scalar(woven0[0][:, : 2 * early], picked0[:, 0, :, :early])
+        gather(picked0[:, 0, 1, :GROUP], 1, 0, GROUP)
+        gather(picked0[:, 0, 1, GROUP:], 1, GROUP, HALF)
+        gather(picked0[:, 1, 1, :], 1, HALF, S)
+        weave_on_scalar(woven0[0][:, : 2 * GROUP], picked0[:, 0, :, :GROUP])
+        weave_on_scalar(woven0[0][:, 2 * GROUP : 2 * early], picked0[:, 0, :, GROUP:early])
 
         round_docs(on_vector, 2, 0, 0, 2 * LATE)
         round_docs(on_vector, 2, 0, SCALAR_OF_PAIR2[1], T)

@@ -14,6 +14,7 @@ U8 = mybir.dt.uint8
 FP8X4 = mybir.dt.float8_e4m3fn_x4
 FP4X4 = mybir.dt.float4_e2m1fn_x4
 SIGMOID = mybir.ActivationFunctionType.Sigmoid
+COPY = mybir.ActivationFunctionType.Copy
 SUBTRACT = mybir.AluOpType.subtract
 
 P = 128
@@ -27,19 +28,10 @@ GROUP = 128
 GROUPS = S // GROUP
 HALF = S // 2
 
-LOADS = [(0, 0, T), (1, 0, T), (2, 0, T), (3, 0, T // 2), (3, T // 2, T)]
-
-SCALAR_OF_PAIR = 352
-SCALAR_OF_LAST = 176
-SCALAR_OF_PAIR2 = (416, 768)
-
-LATE = 32
-OVERLAP = 16
-
 
 def tile_picked_ranknet_sigmoid_e_kernel(tc, xT, w1_words, w1_scales, offs, win, lose, out):
     nc = tc.nc
-    x_rows = xT.rearrange("(z p j) t -> z p j t", p=P, j=PACK)
+    x_rows = xT.rearrange("(z p j) t -> z j p t", p=P, j=PACK)
 
     with ExitStack() as ctx:
         keep = ctx.enter_context(tc.tile_pool(name="keep", bufs=1))
@@ -57,24 +49,12 @@ def tile_picked_ranknet_sigmoid_e_kernel(tc, xT, w1_words, w1_scales, offs, win,
         warm_up = keep.tile([P, 1], F32, name="warm_up")
         nc.scalar.activation(warm_up[:], w_scales_flat.bitcast(F32)[:, 0:1], SIGMOID)
 
-        woven_words = 2 * HALF
-        early = HALF - LATE
-        pair2_at = 2 * early
-        second_half_at = pair2_at + 2 * T - OVERLAP
-        pair3_at = second_half_at + 2 * early
-        shared = keep.tile([P, pair3_at + T], F32, name="shared", align_bytes=64)
-        woven0 = [shared[:, :woven_words], shared[:, second_half_at : second_half_at + woven_words]]
-        rows = {
-            (2, 0): shared[:, pair2_at : pair2_at + 2 * T].rearrange("p (e c) -> p e c", e=2),
-            (3, 0): shared[:, pair3_at:].rearrange("p (e c) -> p e c", e=2),
-        }
-
-        for pair, c0, c1 in LOADS:
-            z, u = divmod(pair, 2)
-            if (pair, c0) not in rows:
-                rows[pair, c0] = keep.tile([P, 2, c1 - c0], F32, name="rows%d_%d" % (pair, c0))[:]
-            nc.sync.dma_start(out=rows[pair, c0], in_=x_rows[z, :, 2 * u : 2 * u + 2, c0:c1])
-            if pair == 0:
+        rows = []
+        for r in range(PASSES * PACK):
+            z, j = divmod(r, PACK)
+            rows.append(keep.tile([P, T], F32, name="row%d" % r))
+            nc.sync.dma_start(out=rows[r][:], in_=x_rows[z, j])
+            if r == 0:
                 nc.sync.dma_start(offs_sb[:], offs)
         for q in range(P // QUADRANT):
             nc.sync.dma_start(
@@ -85,41 +65,39 @@ def tile_picked_ranknet_sigmoid_e_kernel(tc, xT, w1_words, w1_scales, offs, win,
         nc.sync.dma_start(win_sb[:], win)
         nc.sync.dma_start(lose_sb[:], lose)
 
-        group_banks = [psum.tile([P, GROUP], F32, name="group_bank%d" % g) for g in range(GROUPS)]
-        wide_bank = psum.tile([P, S], F32, name="wide_bank")
+        banks = [[psum.tile([P, GROUP], F32, name="bank%d_%d" % (b, g)) for g in range(GROUPS)] for b in range(BLOCKS)]
         y = [keep.tile([P, S], F32, name="y%d" % b) for b in range(BLOCKS)]
         codes = [keep.tile([P, S], U32, name="codes%d" % z, align_bytes=64) for z in range(PASSES)]
         scales = [keep.tile([P, S], U8, name="scales%d" % z, align_bytes=64) for z in range(PASSES)]
-        windows = [keep.tile([P, 2 * T], BF16, name="window%d" % pair, align_bytes=64) for pair in range(2 * PASSES)]
-
-        group_spans = [(GROUP * g, GROUP * (g + 1)) for g in range(GROUPS)]
-        half_spans = [(0, HALF), (HALF, S)]
-        on_scalar, on_vector = nc.scalar.copy, nc.vector.tensor_copy
-
-        def round_docs(copy, pair, load_first, c0, c1):
-            copy(
-                windows[pair][:, 2 * c0 : 2 * c1].rearrange("p (c e) -> p c e", e=2),
-                rows[pair, load_first][:, :, c0 - load_first : c1 - load_first].rearrange("p e c -> p c e"),
-            )
+        planes = [keep.tile([P, PACK * S], BF16, name="planes%d" % z, align_bytes=64) for z in range(PASSES)]
+        woven = [keep.tile([P, PACK * S], BF16, name="woven%d" % z, align_bytes=64) for z in range(PASSES)]
 
         def entries(places, first, end):
             return places[:, first // LIST_ROWS : end // LIST_ROWS]
 
-        def gather(dst, pair, s0, s1):
-            nc.vector.tensor_copy(dst, windows[pair][:].bitcast(U32).indirect(entries(offs_sb, s0, s1)))
+        def gather_on_scalar(dst, window, places, first, end):
+            nc.scalar.activation(dst, window[:].indirect(entries(places, first, end)), COPY)
 
-        def weave_on_scalar(woven, picked):
-            on_scalar(woven.bitcast(U32).rearrange("p (s u) -> p s u", u=2), picked.rearrange("p u s -> p s u"))
+        def gather_on_vector(dst, window, places, first, end):
+            nc.vector.tensor_copy(dst, window[:].indirect(entries(places, first, end)))
 
-        def weave_on_vector(woven, picked):
-            on_vector(woven.bitcast(I32).rearrange("p (s u) -> p s u", u=2), picked.bitcast(I32).rearrange("p u s -> p s u"))
+        def pick(gather, r, s0, s1):
+            z, j = divmod(r, PACK)
+            gather(planes[z][:, S * j + s0 : S * j + s1], rows[r], offs_sb, s0, s1)
 
-        def quantise(z, woven, s0, s1):
-            nc.vector.quantize_mx(out=codes[z][:, s0:s1].bitcast(FP8X4), scales=scales[z][:, s0:s1], in_=woven)
+        def weave(copy, z, s0, s1):
+            copy(
+                woven[z][:, PACK * s0 : PACK * s1].rearrange("p (s j) -> p s j", j=PACK),
+                planes[z][:].rearrange("p (j s) -> p s j", j=PACK)[:, s0:s1, :],
+            )
 
-        def multiply(bank, z, b, s0, s1):
+        def quantise(z, s0, s1):
+            nc.vector.quantize_mx(out=codes[z][:, s0:s1].bitcast(FP8X4), scales=scales[z][:, s0:s1], in_=woven[z][:, PACK * s0 : PACK * s1])
+
+        def multiply(z, b, g):
+            s0, s1 = GROUP * g, GROUP * (g + 1)
             nc.tensor.matmul_mx(
-                out=bank[:],
+                out=banks[b][g][:],
                 lhsT=w_words[:, z, 2 * P * b : 2 * P * (b + 1)].bitcast(FP4X4),
                 lhsT_scale=w_scales[:, z, P * b : P * (b + 1)],
                 rhs=codes[z][:, s0:s1].bitcast(FP8X4),
@@ -128,67 +106,50 @@ def tile_picked_ranknet_sigmoid_e_kernel(tc, xT, w1_words, w1_scales, offs, win,
                 stop=(z == PASSES - 1),
             )
 
-        picked0_tile = keep.tile([P, 2 * S], U32, name="picked0")
-        picked0 = picked0_tile[:].rearrange("p (i u s) -> p i u s", i=2, u=2)
-        round_docs(on_scalar, 0, 0, 0, SCALAR_OF_PAIR)
-        round_docs(on_vector, 0, 0, SCALAR_OF_PAIR, T)
-        gather(picked0[:, :, 0, :], 0, 0, S)
-        round_docs(on_scalar, 1, 0, 0, SCALAR_OF_PAIR)
-        round_docs(on_vector, 1, 0, SCALAR_OF_PAIR, T)
-        gather(picked0[:, 0, 1, :GROUP], 1, 0, GROUP)
-        gather(picked0[:, 0, 1, GROUP:], 1, GROUP, HALF)
-        gather(picked0[:, 1, 1, :], 1, HALF, S)
-        weave_on_scalar(woven0[0][:, : 2 * GROUP], picked0[:, 0, :, :GROUP])
-        weave_on_scalar(woven0[0][:, 2 * GROUP : 2 * early], picked0[:, 0, :, GROUP:early])
+        on_scalar, on_vector = nc.scalar.copy, nc.vector.tensor_copy
 
-        round_docs(on_vector, 2, 0, 0, 2 * LATE)
-        round_docs(on_vector, 2, 0, SCALAR_OF_PAIR2[1], T)
-        round_docs(on_scalar, 2, 0, *SCALAR_OF_PAIR2)
-        weave_on_vector(woven0[0][:, 2 * early :], picked0[:, 0, :, early:])
-        round_docs(on_vector, 2, 0, 2 * LATE, SCALAR_OF_PAIR2[0])
-        weave_on_scalar(woven0[1][:, : 2 * early], picked0[:, 1, :, :early])
-        quantise(0, woven0[0].bitcast(BF16), *half_spans[0])
-        for g in range(GROUPS // 2):
-            multiply(group_banks[g], 0, 0, *group_spans[g])
+        pick(gather_on_scalar, 0, 0, S)
+        pick(gather_on_vector, 1, 0, S)
+        pick(gather_on_scalar, 2, 0, S)
+        pick(gather_on_scalar, 3, 0, HALF)
+        pick(gather_on_vector, 3, HALF, S)
+        weave(on_vector, 0, 0, HALF)
+        weave(on_vector, 0, HALF, S)
+        quantise(0, 0, HALF)
+        quantise(0, HALF, S)
+        for b in range(BLOCKS):
+            for g in range(GROUPS):
+                multiply(0, b, g)
+        pick(gather_on_scalar, 4, 0, S)
+        pick(gather_on_scalar, 5, 0, HALF)
+        pick(gather_on_vector, 5, HALF, S)
+        pick(gather_on_scalar, 6, 0, HALF)
+        pick(gather_on_vector, 6, HALF, S)
 
-        picked1_tile = keep.tile([P, 2 * S], U32, name="picked1", align_bytes=64)
-        picked1 = picked1_tile[:].rearrange("p (g u s) -> p g u s", u=2, s=GROUP)
-        last = GROUPS - 1
-        woven1 = [keep.tile([P, PACK * GROUP], BF16, name="woven1_%d" % g, align_bytes=64)[:] for g in range(last)]
-        woven1.append(picked1_tile[:, 2 * GROUP : 4 * GROUP].bitcast(BF16))
-        gather(picked1[:, :, 0, :], 2, 0, S)
-
-        round_docs(on_scalar, 3, 0, 0, T // 4)
-        round_docs(on_scalar, 3, 0, T // 4, T // 2)
-        weave_on_scalar(woven0[1][:, 2 * early :], picked0[:, 1, :, early:])
-        round_docs(on_scalar, 3, T // 2, T // 2, T // 2 + SCALAR_OF_LAST)
-        round_docs(on_vector, 3, T // 2, T // 2 + SCALAR_OF_LAST, T)
-        quantise(0, woven0[1].bitcast(BF16), *half_spans[1])
-        for g in range(GROUPS // 2, GROUPS):
-            multiply(group_banks[g], 0, 0, *group_spans[g])
-        multiply(wide_bank, 0, 1, 0, S)
-
-        for g, span in enumerate(group_spans):
-            gather(picked1[:, g, 1, :], 3, *span)
-        for g in range(last):
-            weave_on_scalar(woven1[g], picked1[:, g])
-        half_group = GROUP // 2
-        weave_on_scalar(woven1[last][:, : PACK * half_group], picked1[:, last, :, :half_group])
-        for g, (s0, s1) in enumerate(group_spans):
-            if g == last - 1:
-                weave_on_vector(woven1[last][:, PACK * half_group :], picked1[:, last, :, half_group:])
-            quantise(1, woven1[g], s0, s1)
-            multiply(group_banks[g], 1, 0, s0, s1)
-            nc.scalar.copy(y[0][:, s0:s1], group_banks[g][:])
-        multiply(wide_bank, 1, 1, 0, S)
-        nc.scalar.copy(y[1][:], wide_bank[:])
+        spans = [(GROUP * g, GROUP * (g + 1)) for g in range(GROUPS)]
+        pick(gather_on_vector, 7, *spans[3])
+        for g in range(3):
+            pick(gather_on_scalar, 7, *spans[g])
+        weave(on_vector, 1, *spans[0])
+        weave(on_vector, 1, *spans[1])
+        weave(on_scalar, 1, *spans[3])
+        quantise(1, *spans[0])
+        weave(on_vector, 1, *spans[2])
+        for g in range(GROUPS):
+            if g > 0:
+                quantise(1, *spans[g])
+            for b in range(BLOCKS):
+                multiply(1, b, g)
+            for b in range(BLOCKS):
+                copy = on_vector if (g, b) == (GROUPS - 1, 0) else on_scalar
+                copy(y[b][:, spans[g][0] : spans[g][1]], banks[b][g][:])
 
         lost = [keep.tile([P, V], F32, name="lost%d" % b) for b in range(BLOCKS)]
         margin = [keep.tile([P, V], F32, name="margin%d" % b) for b in range(BLOCKS)]
         result = [keep.tile([P, V], F32, name="result%d" % b) for b in range(BLOCKS)]
 
-        def fetch_losers(b, v0, v1):
-            nc.vector.tensor_copy(lost[b][:, v0:v1], y[b][:].indirect(entries(lose_sb, v0, v1)))
+        def fetch_losers(gather, b, v0, v1):
+            gather(lost[b][:, v0:v1], y[b], lose_sb, v0, v1)
 
         def subtract(b, v0, v1):
             nc.vector.tensor_tensor(margin[b][:, v0:v1], y[b][:].indirect(entries(win_sb, v0, v1)), lost[b][:, v0:v1], SUBTRACT)
@@ -197,14 +158,15 @@ def tile_picked_ranknet_sigmoid_e_kernel(tc, xT, w1_words, w1_scales, offs, win,
             nc.scalar.activation(result[b][:, v0:v1], margin[b][:, v0:v1], SIGMOID)
             nc.sync.dma_start(out=out[P * b : P * (b + 1), v0:v1], in_=result[b][:, v0:v1])
 
-        compared_halves = [(0, V // 2), (V // 2, V)]
-        for half in compared_halves:
-            fetch_losers(0, *half)
-        for half in compared_halves:
-            subtract(0, *half)
+        first, second = (0, V // 2), (V // 2, V)
+        fetch_losers(gather_on_vector, 0, *first)
+        fetch_losers(gather_on_scalar, 0, *second)
+        fetch_losers(gather_on_scalar, 1, *first)
+        fetch_losers(gather_on_scalar, 1, *second)
+        subtract(0, *second)
+        subtract(0, *first)
         finish(0, 0, V)
-        for half in compared_halves:
-            fetch_losers(1, *half)
-        for half in compared_halves:
-            subtract(1, *half)
-            finish(1, *half)
+        subtract(1, *first)
+        finish(1, *first)
+        subtract(1, *second)
+        finish(1, *second)

@@ -44,7 +44,7 @@ def tile_picked_ranknet_sigmoid_e_kernel(tc, xT, w1_words, w1_scales, offs, win,
         w_scales = keep.tile([P, PASSES, N], U8, name="w_scales", align_bytes=64)
         w_scales_flat = w_scales[:].rearrange("p z n -> p (z n)")
         nc.vector.memset(w_scales_flat.bitcast(I32), 0)
-        w_words = keep.tile([P, PASSES, 2 * N], U8, name="w_words", align_bytes=64)
+        w_words = [keep.tile([P, 2 * N], U8, name="w_words%d" % z, align_bytes=64) for z in range(PASSES)]
 
         warm_up = keep.tile([P, 1], F32, name="warm_up")
         nc.scalar.activation(warm_up[:], w_scales_flat.bitcast(F32)[:, 0:1], SIGMOID)
@@ -56,12 +56,14 @@ def tile_picked_ranknet_sigmoid_e_kernel(tc, xT, w1_words, w1_scales, offs, win,
             nc.sync.dma_start(out=rows[r][:], in_=x_rows[z, j])
             if r == 0:
                 nc.sync.dma_start(offs_sb[:], offs)
-        for q in range(P // QUADRANT):
-            nc.sync.dma_start(
-                out=w_scales[QUADRANT * q : QUADRANT * q + SCALE_ROWS].bitcast(I32),
-                in_=w1_scales[:, SCALE_ROWS * q : SCALE_ROWS * (q + 1), :].rearrange("z r n -> r z n").bitcast(I32),
-            )
-        nc.sync.dma_start(out=w_words[:], in_=w1_words.rearrange("z p n -> p z n"))
+            if r == PASSES * PACK - 2:
+                for q in range(P // QUADRANT):
+                    nc.sync.dma_start(
+                        out=w_scales[QUADRANT * q : QUADRANT * q + SCALE_ROWS].bitcast(I32),
+                        in_=w1_scales[:, SCALE_ROWS * q : SCALE_ROWS * (q + 1), :].rearrange("z r n -> r z n").bitcast(I32),
+                    )
+                nc.sync.dma_start(out=w_words[0][:], in_=w1_words[0])
+        nc.sync.dma_start(out=w_words[1][:], in_=w1_words[1])
         nc.sync.dma_start(win_sb[:], win)
         nc.sync.dma_start(lose_sb[:], lose)
 
@@ -85,10 +87,10 @@ def tile_picked_ranknet_sigmoid_e_kernel(tc, xT, w1_words, w1_scales, offs, win,
             z, j = divmod(r, PACK)
             gather(planes[z][:, S * j + s0 : S * j + s1], rows[r], offs_sb, s0, s1)
 
-        def weave(copy, z, s0, s1):
+        def weave(copy, z, j0, j1, s0, s1):
             copy(
-                woven[z][:, PACK * s0 : PACK * s1].rearrange("p (s j) -> p s j", j=PACK),
-                planes[z][:].rearrange("p (j s) -> p s j", j=PACK)[:, s0:s1, :],
+                woven[z][:, PACK * s0 : PACK * s1].rearrange("p (s j) -> p s j", j=PACK)[:, :, j0:j1],
+                planes[z][:].rearrange("p (j s) -> p s j", j=PACK)[:, s0:s1, j0:j1],
             )
 
         def quantise(z, s0, s1):
@@ -98,7 +100,7 @@ def tile_picked_ranknet_sigmoid_e_kernel(tc, xT, w1_words, w1_scales, offs, win,
             s0, s1 = GROUP * g, GROUP * (g + 1)
             nc.tensor.matmul_mx(
                 out=banks[b][g][:],
-                lhsT=w_words[:, z, 2 * P * b : 2 * P * (b + 1)].bitcast(FP4X4),
+                lhsT=w_words[z][:, 2 * P * b : 2 * P * (b + 1)].bitcast(FP4X4),
                 lhsT_scale=w_scales[:, z, P * b : P * (b + 1)],
                 rhs=codes[z][:, s0:s1].bitcast(FP8X4),
                 rhs_scale=scales[z][:, s0:s1],
@@ -108,40 +110,43 @@ def tile_picked_ranknet_sigmoid_e_kernel(tc, xT, w1_words, w1_scales, offs, win,
 
         on_scalar, on_vector = nc.scalar.copy, nc.vector.tensor_copy
 
-        pick(gather_on_scalar, 0, 0, S)
-        pick(gather_on_vector, 1, 0, S)
+        for r in range(2):
+            pick(gather_on_scalar, r, 0, HALF)
+            pick(gather_on_vector, r, HALF, S)
+        weave(on_vector, 0, 0, 2, 0, S)
         pick(gather_on_scalar, 2, 0, S)
-        pick(gather_on_scalar, 3, 0, HALF)
-        pick(gather_on_vector, 3, HALF, S)
-        weave(on_vector, 0, 0, HALF)
-        weave(on_vector, 0, HALF, S)
+        pick(gather_on_vector, 3, 0, HALF)
+        pick(gather_on_scalar, 3, HALF, S)
+        weave(on_vector, 0, 2, PACK, 0, HALF)
+        weave(on_vector, 0, 2, PACK, HALF, S)
         quantise(0, 0, HALF)
         quantise(0, HALF, S)
-        for b in range(BLOCKS):
-            for g in range(GROUPS):
+        for g in range(GROUPS):
+            for b in range(BLOCKS):
                 multiply(0, b, g)
         pick(gather_on_scalar, 4, 0, S)
         pick(gather_on_scalar, 5, 0, HALF)
         pick(gather_on_vector, 5, HALF, S)
-        pick(gather_on_scalar, 6, 0, HALF)
-        pick(gather_on_vector, 6, HALF, S)
+        weave(on_vector, 1, 0, 2, 0, HALF)
+        weave(on_vector, 1, 0, 2, HALF, S)
+        pick(gather_on_scalar, 6, 0, S)
 
         spans = [(GROUP * g, GROUP * (g + 1)) for g in range(GROUPS)]
-        pick(gather_on_vector, 7, *spans[3])
-        for g in range(3):
+        pick(gather_on_vector, 7, *spans[0])
+        for g in range(1, GROUPS):
             pick(gather_on_scalar, 7, *spans[g])
-        weave(on_vector, 1, *spans[0])
-        weave(on_vector, 1, *spans[1])
-        weave(on_scalar, 1, *spans[3])
+        weave(on_vector, 1, 2, PACK, *spans[0])
+        weave(on_vector, 1, 2, PACK, *spans[1])
         quantise(1, *spans[0])
-        weave(on_vector, 1, *spans[2])
+        weave(on_scalar, 1, 2, PACK, *spans[2])
+        weave(on_vector, 1, 2, PACK, *spans[3])
         for g in range(GROUPS):
             if g > 0:
                 quantise(1, *spans[g])
             for b in range(BLOCKS):
                 multiply(1, b, g)
             for b in range(BLOCKS):
-                copy = on_vector if (g, b) == (GROUPS - 1, 0) else on_scalar
+                copy = on_vector if (g, b) == (3, 0) else on_scalar
                 copy(y[b][:, spans[g][0] : spans[g][1]], banks[b][g][:])
 
         lost = [keep.tile([P, V], F32, name="lost%d" % b) for b in range(BLOCKS)]
@@ -159,14 +164,16 @@ def tile_picked_ranknet_sigmoid_e_kernel(tc, xT, w1_words, w1_scales, offs, win,
             nc.sync.dma_start(out=out[P * b : P * (b + 1), v0:v1], in_=result[b][:, v0:v1])
 
         first, second = (0, V // 2), (V // 2, V)
+        won = keep.tile([P, V // 2], F32, name="won")
         fetch_losers(gather_on_vector, 0, *first)
         fetch_losers(gather_on_scalar, 0, *second)
         fetch_losers(gather_on_scalar, 1, *first)
         fetch_losers(gather_on_scalar, 1, *second)
+        gather_on_scalar(won[:], y[1], win_sb, *second)
         subtract(0, *second)
         subtract(0, *first)
         finish(0, 0, V)
         subtract(1, *first)
         finish(1, *first)
-        subtract(1, *second)
+        nc.vector.tensor_tensor(margin[1][:, V // 2 :], won[:], lost[1][:, V // 2 :], SUBTRACT)
         finish(1, *second)

@@ -27,11 +27,12 @@ LIST_ROWS = 16
 GROUP = 128
 GROUPS = S // GROUP
 HALF = S // 2
+LOADS = [(0, 2), (2, 2), (4, 2), (6, 1), (7, 1)]
 
 
 def tile_picked_ranknet_sigmoid_e_kernel(tc, xT, w1_words, w1_scales, offs, win, lose, out):
     nc = tc.nc
-    x_rows = xT.rearrange("(z p j) t -> z j p t", p=P, j=PACK)
+    x_rows = xT.rearrange("(z p j) t -> z p (j t)", p=P, j=PACK)
 
     with ExitStack() as ctx:
         keep = ctx.enter_context(tc.tile_pool(name="keep", bufs=1))
@@ -44,26 +45,25 @@ def tile_picked_ranknet_sigmoid_e_kernel(tc, xT, w1_words, w1_scales, offs, win,
         w_scales = keep.tile([P, PASSES, N], U8, name="w_scales", align_bytes=64)
         w_scales_flat = w_scales[:].rearrange("p z n -> p (z n)")
         nc.vector.memset(w_scales_flat.bitcast(I32), 0)
-        w_words = [keep.tile([P, 2 * N], U8, name="w_words%d" % z, align_bytes=64) for z in range(PASSES)]
+        w_words = keep.tile([P, PASSES, 2 * N], U8, name="w_words", align_bytes=64)
 
         warm_up = keep.tile([P, 1], F32, name="warm_up")
         nc.scalar.activation(warm_up[:], w_scales_flat.bitcast(F32)[:, 0:1], SIGMOID)
 
         rows = []
-        for r in range(PASSES * PACK):
-            z, j = divmod(r, PACK)
-            rows.append(keep.tile([P, T], F32, name="row%d" % r))
-            nc.sync.dma_start(out=rows[r][:], in_=x_rows[z, j])
-            if r == 0:
+        for first, count in LOADS:
+            z, j = divmod(first, PACK)
+            loaded = keep.tile([P, count * T], F32, name="loaded%d" % first)
+            nc.sync.dma_start(out=loaded[:], in_=x_rows[z, :, j * T : (j + count) * T])
+            rows.extend([loaded[:, T * i : T * (i + 1)] for i in range(count)])
+            if first == 0:
                 nc.sync.dma_start(offs_sb[:], offs)
-            if r == PASSES * PACK - 2:
-                for q in range(P // QUADRANT):
-                    nc.sync.dma_start(
-                        out=w_scales[QUADRANT * q : QUADRANT * q + SCALE_ROWS].bitcast(I32),
-                        in_=w1_scales[:, SCALE_ROWS * q : SCALE_ROWS * (q + 1), :].rearrange("z r n -> r z n").bitcast(I32),
-                    )
-                nc.sync.dma_start(out=w_words[0][:], in_=w1_words[0])
-        nc.sync.dma_start(out=w_words[1][:], in_=w1_words[1])
+        for q in range(P // QUADRANT):
+            nc.sync.dma_start(
+                out=w_scales[QUADRANT * q : QUADRANT * q + SCALE_ROWS].bitcast(I32),
+                in_=w1_scales[:, SCALE_ROWS * q : SCALE_ROWS * (q + 1), :].rearrange("z r n -> r z n").bitcast(I32),
+            )
+        nc.sync.dma_start(out=w_words[:], in_=w1_words.rearrange("z p n -> p z n"))
         nc.sync.dma_start(win_sb[:], win)
         nc.sync.dma_start(lose_sb[:], lose)
 
@@ -71,17 +71,17 @@ def tile_picked_ranknet_sigmoid_e_kernel(tc, xT, w1_words, w1_scales, offs, win,
         y = [keep.tile([P, S], F32, name="y%d" % b) for b in range(BLOCKS)]
         codes = [keep.tile([P, S], U32, name="codes%d" % z, align_bytes=64) for z in range(PASSES)]
         scales = [keep.tile([P, S], U8, name="scales%d" % z, align_bytes=64) for z in range(PASSES)]
-        planes = [keep.tile([P, PACK * S], BF16, name="planes%d" % z, align_bytes=64) for z in range(PASSES)]
+        planes = [keep.tile([P, PACK * S], F32, name="planes%d" % z, align_bytes=64) for z in range(PASSES)]
         woven = [keep.tile([P, PACK * S], BF16, name="woven%d" % z, align_bytes=64) for z in range(PASSES)]
 
         def entries(places, first, end):
             return places[:, first // LIST_ROWS : end // LIST_ROWS]
 
         def gather_on_scalar(dst, window, places, first, end):
-            nc.scalar.activation(dst, window[:].indirect(entries(places, first, end)), COPY)
+            nc.scalar.activation(dst, window.indirect(entries(places, first, end)), COPY)
 
         def gather_on_vector(dst, window, places, first, end):
-            nc.vector.tensor_copy(dst, window[:].indirect(entries(places, first, end)))
+            nc.vector.tensor_copy(dst, window.indirect(entries(places, first, end)))
 
         def pick(gather, r, s0, s1):
             z, j = divmod(r, PACK)
@@ -100,7 +100,7 @@ def tile_picked_ranknet_sigmoid_e_kernel(tc, xT, w1_words, w1_scales, offs, win,
             s0, s1 = GROUP * g, GROUP * (g + 1)
             nc.tensor.matmul_mx(
                 out=banks[b][g][:],
-                lhsT=w_words[z][:, 2 * P * b : 2 * P * (b + 1)].bitcast(FP4X4),
+                lhsT=w_words[:, z, 2 * P * b : 2 * P * (b + 1)].bitcast(FP4X4),
                 lhsT_scale=w_scales[:, z, P * b : P * (b + 1)],
                 rhs=codes[z][:, s0:s1].bitcast(FP8X4),
                 rhs_scale=scales[z][:, s0:s1],
@@ -110,51 +110,51 @@ def tile_picked_ranknet_sigmoid_e_kernel(tc, xT, w1_words, w1_scales, offs, win,
 
         on_scalar, on_vector = nc.scalar.copy, nc.vector.tensor_copy
 
-        for r in range(2):
-            pick(gather_on_scalar, r, 0, HALF)
-            pick(gather_on_vector, r, HALF, S)
+        spans = [(GROUP * g, GROUP * (g + 1)) for g in range(GROUPS)]
+
+        def copy_out(copy, b, g):
+            copy(y[b][:, spans[g][0] : spans[g][1]], banks[b][g][:])
+
+        pick(gather_on_scalar, 0, 0, S)
+        pick(gather_on_vector, 1, 0, S)
         weave(on_vector, 0, 0, 2, 0, S)
-        pick(gather_on_scalar, 2, 0, S)
-        pick(gather_on_vector, 3, 0, HALF)
-        pick(gather_on_scalar, 3, HALF, S)
-        weave(on_vector, 0, 2, PACK, 0, HALF)
+        for half in ((0, HALF), (HALF, S)):
+            pick(gather_on_scalar, 2, *half)
+            pick(gather_on_vector, 3, *half)
+        weave(on_scalar, 0, 2, PACK, 0, 160)
+        weave(on_vector, 0, 2, PACK, 160, HALF)
         weave(on_vector, 0, 2, PACK, HALF, S)
         quantise(0, 0, HALF)
         quantise(0, HALF, S)
-        for g in range(GROUPS):
-            for b in range(BLOCKS):
-                multiply(0, b, g)
         pick(gather_on_scalar, 4, 0, S)
-        pick(gather_on_scalar, 5, 0, HALF)
-        pick(gather_on_vector, 5, HALF, S)
-        weave(on_vector, 1, 0, 2, 0, HALF)
-        weave(on_vector, 1, 0, 2, HALF, S)
-        pick(gather_on_scalar, 6, 0, S)
+        pick(gather_on_vector, 5, 0, S)
+        pick(gather_on_scalar, 6, 0, 384)
+        pick(gather_on_vector, 6, 384, S)
 
-        spans = [(GROUP * g, GROUP * (g + 1)) for g in range(GROUPS)]
-        pick(gather_on_vector, 7, *spans[0])
-        for g in range(1, GROUPS):
-            pick(gather_on_scalar, 7, *spans[g])
-        weave(on_vector, 1, 2, PACK, *spans[0])
-        weave(on_vector, 1, 2, PACK, *spans[1])
-        quantise(1, *spans[0])
-        weave(on_scalar, 1, 2, PACK, *spans[2])
-        weave(on_vector, 1, 2, PACK, *spans[3])
         for g in range(GROUPS):
-            if g > 0:
-                quantise(1, *spans[g])
-            for b in range(BLOCKS):
-                multiply(1, b, g)
-            for b in range(BLOCKS):
-                copy = on_vector if (g, b) == (3, 0) else on_scalar
-                copy(y[b][:, spans[g][0] : spans[g][1]], banks[b][g][:])
+            pick(gather_on_vector if g < 2 else gather_on_scalar, 7, *spans[g])
+        weave(on_vector, 1, 0, PACK, *spans[0])
+        weave(on_vector, 1, 0, PACK, *spans[1])
+        quantise(1, *spans[0])
+        weave(on_scalar, 1, 0, PACK, *spans[2])
+        weave(on_scalar, 1, 0, PACK, 384, 448)
+        weave(on_vector, 1, 0, PACK, 448, S)
+        for g in range(1, GROUPS):
+            quantise(1, *spans[g])
+
+        for b in range(BLOCKS):
+            for g in range(GROUPS):
+                multiply(0, b, g)
+        for b, g in ((0, 0), (0, 1), (1, 0), (0, 2), (0, 3), (1, 1), (1, 2), (1, 3)):
+            multiply(1, b, g)
+            copy_out(on_vector if (b, g) == (0, 3) else on_scalar, b, g)
 
         lost = [keep.tile([P, V], F32, name="lost%d" % b) for b in range(BLOCKS)]
         margin = [keep.tile([P, V], F32, name="margin%d" % b) for b in range(BLOCKS)]
         result = [keep.tile([P, V], F32, name="result%d" % b) for b in range(BLOCKS)]
 
         def fetch_losers(gather, b, v0, v1):
-            gather(lost[b][:, v0:v1], y[b], lose_sb, v0, v1)
+            gather(lost[b][:, v0:v1], y[b][:], lose_sb, v0, v1)
 
         def subtract(b, v0, v1):
             nc.vector.tensor_tensor(margin[b][:, v0:v1], y[b][:].indirect(entries(win_sb, v0, v1)), lost[b][:, v0:v1], SUBTRACT)
@@ -164,16 +164,16 @@ def tile_picked_ranknet_sigmoid_e_kernel(tc, xT, w1_words, w1_scales, offs, win,
             nc.sync.dma_start(out=out[P * b : P * (b + 1), v0:v1], in_=result[b][:, v0:v1])
 
         first, second = (0, V // 2), (V // 2, V)
-        won = keep.tile([P, V // 2], F32, name="won")
+        won = [keep.tile([P, V // 2], F32, name="won%d" % b) for b in range(1)]
         fetch_losers(gather_on_vector, 0, *first)
         fetch_losers(gather_on_scalar, 0, *second)
+        gather_on_vector(won[0][:], y[0][:], win_sb, *second)
         fetch_losers(gather_on_scalar, 1, *first)
         fetch_losers(gather_on_scalar, 1, *second)
-        gather_on_scalar(won[:], y[1], win_sb, *second)
-        subtract(0, *second)
         subtract(0, *first)
+        nc.vector.tensor_tensor(margin[0][:, V // 2 :], won[0][:], lost[0][:, V // 2 :], SUBTRACT)
         finish(0, 0, V)
         subtract(1, *first)
         finish(1, *first)
-        nc.vector.tensor_tensor(margin[1][:, V // 2 :], won[:], lost[1][:, V // 2 :], SUBTRACT)
+        subtract(1, *second)
         finish(1, *second)

@@ -87,10 +87,10 @@ def tile_picked_ranknet_sigmoid_e_kernel(tc, xT, w1_words, w1_scales, offs, win,
             z, j = divmod(r, PACK)
             gather(planes[z][:, S * j + s0 : S * j + s1], rows[r], offs_sb, s0, s1)
 
-        def weave(copy, z, j0, j1, s0, s1):
+        def weave_by_lines(copy, s0, s1, z=1):
             copy(
-                woven[z][:, PACK * s0 : PACK * s1].rearrange("p (s j) -> p s j", j=PACK)[:, :, j0:j1],
-                planes[z][:].rearrange("p (j s) -> p s j", j=PACK)[:, s0:s1, j0:j1],
+                woven[z][:, PACK * s0 : PACK * s1].rearrange("p (c i j) -> p c j i", i=4, j=PACK),
+                planes[z][:].rearrange("p (j s) -> p j s", j=PACK)[:, :, s0:s1].rearrange("p j (c i) -> p c j i", i=4),
             )
 
         def quantise(z, s0, s1):
@@ -117,13 +117,12 @@ def tile_picked_ranknet_sigmoid_e_kernel(tc, xT, w1_words, w1_scales, offs, win,
 
         pick(gather_on_scalar, 0, 0, S)
         pick(gather_on_vector, 1, 0, S)
-        weave(on_vector, 0, 0, 2, 0, S)
         for half in ((0, HALF), (HALF, S)):
             pick(gather_on_scalar, 2, *half)
             pick(gather_on_vector, 3, *half)
-        weave(on_scalar, 0, 2, PACK, 0, 160)
-        weave(on_vector, 0, 2, PACK, 160, HALF)
-        weave(on_vector, 0, 2, PACK, HALF, S)
+        weave_by_lines(on_scalar, *spans[0], 0)
+        weave_by_lines(on_vector, *spans[1], 0)
+        weave_by_lines(on_vector, HALF, S, 0)
         quantise(0, 0, HALF)
         quantise(0, HALF, S)
         pick(gather_on_scalar, 4, 0, S)
@@ -133,12 +132,12 @@ def tile_picked_ranknet_sigmoid_e_kernel(tc, xT, w1_words, w1_scales, offs, win,
 
         for g in range(GROUPS):
             pick(gather_on_vector if g < 2 else gather_on_scalar, 7, *spans[g])
-        weave(on_vector, 1, 0, PACK, *spans[0])
-        weave(on_vector, 1, 0, PACK, *spans[1])
+        weave_by_lines(on_vector, *spans[0])
+        weave_by_lines(on_vector, *spans[1])
         quantise(1, *spans[0])
-        weave(on_scalar, 1, 0, PACK, *spans[2])
-        weave(on_scalar, 1, 0, PACK, 384, 448)
-        weave(on_vector, 1, 0, PACK, 448, S)
+        weave_by_lines(on_scalar, *spans[2])
+        weave_by_lines(on_scalar, 384, 448)
+        weave_by_lines(on_vector, 448, S)
         for g in range(1, GROUPS):
             quantise(1, *spans[g])
 

@@ -144,7 +144,7 @@ def tile_picked_ranknet_sigmoid_e_kernel(tc, xT, w1_words, w1_scales, offs, win,
         for b in range(BLOCKS):
             for g in range(GROUPS):
                 multiply(0, b, g)
-        for b, g in ((0, 0), (0, 1), (1, 0), (0, 2), (0, 3), (1, 1), (1, 2), (1, 3)):
+        for b, g in ((0, 0), (1, 0), (0, 1), (0, 2), (0, 3), (1, 1), (1, 2), (1, 3)):
             multiply(1, b, g)
             copy_out(on_vector if (b, g) == (0, 3) else on_scalar, b, g)
 
@@ -169,10 +169,14 @@ def tile_picked_ranknet_sigmoid_e_kernel(tc, xT, w1_words, w1_scales, offs, win,
         gather_on_vector(won[0][:], y[0][:], win_sb, *second)
         fetch_losers(gather_on_scalar, 1, *first)
         fetch_losers(gather_on_scalar, 1, *second)
+        tail = 192
+        won_last = keep.tile([P, V - tail], F32, name="won_last")
+        gather_on_scalar(won_last[:], y[1][:], win_sb, tail, V)
         subtract(0, *first)
         nc.vector.tensor_tensor(margin[0][:, V // 2 :], won[0][:], lost[0][:, V // 2 :], SUBTRACT)
         finish(0, 0, V)
         subtract(1, *first)
         finish(1, *first)
-        subtract(1, *second)
+        subtract(1, V // 2, tail)
+        nc.vector.tensor_tensor(margin[1][:, tail:], won_last[:], lost[1][:, tail:], SUBTRACT)
         finish(1, *second)

@@ -178,5 +178,7 @@ def tile_picked_ranknet_sigmoid_e_kernel(tc, xT, w1_words, w1_scales, offs, win,
         subtract(1, *first)
         finish(1, *first)
         subtract(1, V // 2, tail)
+        nc.scalar.activation(result[1][:, V // 2 : tail], margin[1][:, V // 2 : tail], SIGMOID)
         nc.vector.tensor_tensor(margin[1][:, tail:], won_last[:], lost[1][:, tail:], SUBTRACT)
-        finish(1, *second)
+        nc.scalar.activation(result[1][:, tail:], margin[1][:, tail:], SIGMOID)
+        nc.sync.dma_start(out=out[P:, V // 2 :], in_=result[1][:, V // 2 :])

@@ -45,7 +45,7 @@ def tile_picked_ranknet_sigmoid_e_kernel(tc, xT, w1_words, w1_scales, offs, win,
         w_scales = keep.tile([P, PASSES, N], U8, name="w_scales", align_bytes=64)
         w_scales_flat = w_scales[:].rearrange("p z n -> p (z n)")
         nc.vector.memset(w_scales_flat.bitcast(I32), 0)
-        w_words = keep.tile([P, PASSES, 2 * N], U8, name="w_words", align_bytes=64)
+        w_words = [keep.tile([P, 2 * N], U8, name="w_words%d" % z, align_bytes=64) for z in range(PASSES)]
 
         warm_up = keep.tile([P, 1], F32, name="warm_up")
         nc.scalar.activation(warm_up[:], w_scales_flat.bitcast(F32)[:, 0:1], SIGMOID)
@@ -63,9 +63,10 @@ def tile_picked_ranknet_sigmoid_e_kernel(tc, xT, w1_words, w1_scales, offs, win,
                 out=w_scales[QUADRANT * q : QUADRANT * q + SCALE_ROWS].bitcast(I32),
                 in_=w1_scales[:, SCALE_ROWS * q : SCALE_ROWS * (q + 1), :].rearrange("z r n -> r z n").bitcast(I32),
             )
-        nc.sync.dma_start(out=w_words[:], in_=w1_words.rearrange("z p n -> p z n"))
-        nc.sync.dma_start(win_sb[:], win)
+        for z in range(PASSES):
+            nc.sync.dma_start(out=w_words[z][:], in_=w1_words[z])
         nc.sync.dma_start(lose_sb[:], lose)
+        nc.sync.dma_start(win_sb[:], win)
 
         banks = [[psum.tile([P, GROUP], F32, name="bank%d_%d" % (b, g)) for g in range(GROUPS)] for b in range(BLOCKS)]
         y = [keep.tile([P, S], F32, name="y%d" % b) for b in range(BLOCKS)]
@@ -100,7 +101,7 @@ def tile_picked_ranknet_sigmoid_e_kernel(tc, xT, w1_words, w1_scales, offs, win,
             s0, s1 = GROUP * g, GROUP * (g + 1)
             nc.tensor.matmul_mx(
                 out=banks[b][g][:],
-                lhsT=w_words[:, z, 2 * P * b : 2 * P * (b + 1)].bitcast(FP4X4),
+                lhsT=w_words[z][:, 2 * P * b : 2 * P * (b + 1)].bitcast(FP4X4),
                 lhsT_scale=w_scales[:, z, P * b : P * (b + 1)],
                 rhs=codes[z][:, s0:s1].bitcast(FP8X4),
                 rhs_scale=scales[z][:, s0:s1],
@@ -176,9 +177,9 @@ def tile_picked_ranknet_sigmoid_e_kernel(tc, xT, w1_words, w1_scales, offs, win,
         nc.vector.tensor_tensor(margin[0][:, V // 2 :], won[0][:], lost[0][:, V // 2 :], SUBTRACT)
         finish(0, 0, V)
         subtract(1, *first)
-        finish(1, *first)
+        nc.scalar.activation(result[1][:, : V // 2], margin[1][:, : V // 2], SIGMOID)
         subtract(1, V // 2, tail)
         nc.scalar.activation(result[1][:, V // 2 : tail], margin[1][:, V // 2 : tail], SIGMOID)
         nc.vector.tensor_tensor(margin[1][:, tail:], won_last[:], lost[1][:, tail:], SUBTRACT)
         nc.scalar.activation(result[1][:, tail:], margin[1][:, tail:], SIGMOID)
-        nc.sync.dma_start(out=out[P:, V // 2 :], in_=result[1][:, V // 2 :])
+        nc.sync.dma_start(out=out[P:, :], in_=result[1][:])

@@ -27,12 +27,11 @@ LIST_ROWS = 16
 GROUP = 128
 GROUPS = S // GROUP
 HALF = S // 2
-LOADS = [(0, 2), (2, 2), (4, 2), (6, 1), (7, 1)]
 
 
 def tile_picked_ranknet_sigmoid_e_kernel(tc, xT, w1_words, w1_scales, offs, win, lose, out):
     nc = tc.nc
-    x_rows = xT.rearrange("(z p j) t -> z p (j t)", p=P, j=PACK)
+    x_rows = xT.rearrange("(z p j) t -> z p j t", p=P, j=PACK)
 
     with ExitStack() as ctx:
         keep = ctx.enter_context(tc.tile_pool(name="keep", bufs=1))
@@ -51,20 +50,20 @@ def tile_picked_ranknet_sigmoid_e_kernel(tc, xT, w1_words, w1_scales, offs, win,
         nc.scalar.activation(warm_up[:], w_scales_flat.bitcast(F32)[:, 0:1], SIGMOID)
 
         rows = []
-        for first, count in LOADS:
-            z, j = divmod(first, PACK)
-            loaded = keep.tile([P, count * T], F32, name="loaded%d" % first)
-            nc.sync.dma_start(out=loaded[:], in_=x_rows[z, :, j * T : (j + count) * T])
-            rows.extend([loaded[:, T * i : T * (i + 1)] for i in range(count)])
-            if first == 0:
+        for source in (x_rows[0, :, 0:2], x_rows[0, :, 2:4], x_rows[1, :, 0:2], x_rows[1, :, 2:3], x_rows[1, :, 3:4]):
+            count = source.shape[1]
+            loaded = keep.tile([P, count * T], F32, name="loaded%d" % len(rows))
+            nc.sync.dma_start(out=loaded[:].rearrange("p (j t) -> p j t", j=count), in_=source)
+            if not rows:
                 nc.sync.dma_start(offs_sb[:], offs)
+            rows.extend([loaded[:, T * i : T * (i + 1)] for i in range(count)])
         for q in range(P // QUADRANT):
             nc.sync.dma_start(
                 out=w_scales[QUADRANT * q : QUADRANT * q + SCALE_ROWS].bitcast(I32),
                 in_=w1_scales[:, SCALE_ROWS * q : SCALE_ROWS * (q + 1), :].rearrange("z r n -> r z n").bitcast(I32),
             )
-        for z in range(PASSES):
-            nc.sync.dma_start(out=w_words[z][:], in_=w1_words[z])
+        nc.sync.dma_start(out=w_words[0][:], in_=w1_words[0])
+        nc.sync.dma_start(out=w_words[1][:], in_=w1_words[1])
         nc.sync.dma_start(lose_sb[:], lose)
         nc.sync.dma_start(win_sb[:], win)
 
@@ -72,7 +71,8 @@ def tile_picked_ranknet_sigmoid_e_kernel(tc, xT, w1_words, w1_scales, offs, win,
         y = [keep.tile([P, S], F32, name="y%d" % b) for b in range(BLOCKS)]
         codes = [keep.tile([P, S], U32, name="codes%d" % z, align_bytes=64) for z in range(PASSES)]
         scales = [keep.tile([P, S], U8, name="scales%d" % z, align_bytes=64) for z in range(PASSES)]
-        planes = [keep.tile([P, PACK * S], F32, name="planes%d" % z, align_bytes=64) for z in range(PASSES)]
+        pairs = [keep.tile([P, 2, 2, GROUP, 2], BF16, name="pairs%d" % z, align_bytes=64) for z in range(PASSES)]
+        planes = [keep.tile([P, PACK, HALF], F32, name="planes%d" % z, align_bytes=64) for z in range(PASSES)]
         woven = [keep.tile([P, PACK * S], BF16, name="woven%d" % z, align_bytes=64) for z in range(PASSES)]
 
         def entries(places, first, end):
@@ -84,20 +84,31 @@ def tile_picked_ranknet_sigmoid_e_kernel(tc, xT, w1_words, w1_scales, offs, win,
         def gather_on_vector(dst, window, places, first, end):
             nc.vector.tensor_copy(dst, window.indirect(entries(places, first, end)))
 
-        def pick(gather, r, s0, s1):
+        def pick_paired(r, g0, g1):
             z, j = divmod(r, PACK)
-            gather(planes[z][:, S * j + s0 : S * j + s1], rows[r], offs_sb, s0, s1)
+            gather_on_vector(pairs[z][:, g0:g1, j // 2, :, j % 2], rows[r], offs_sb, GROUP * g0, GROUP * g1)
 
-        def weave_by_lines(copy, s0, s1, z=1):
-            copy(
-                woven[z][:, PACK * s0 : PACK * s1].rearrange("p (c i j) -> p c j i", i=4, j=PACK),
-                planes[z][:].rearrange("p (j s) -> p j s", j=PACK)[:, :, s0:s1].rearrange("p j (c i) -> p c j i", i=4),
+        def pick_plain(r, s0, s1):
+            z, j = divmod(r, PACK)
+            gather_on_scalar(planes[z][:, j, s0 - HALF : s1 - HALF], rows[r], offs_sb, s0, s1)
+
+        def join(z, g):
+            nc.vector.tensor_copy(
+                woven[z][:, PACK * GROUP * g : PACK * GROUP * (g + 1)].bitcast(I32).rearrange("p (s u) -> p s u", u=2),
+                pairs[z][:, g].rearrange("p u s e -> p (u s e)").bitcast(I32).rearrange("p (u s) -> p s u", u=2),
             )
 
-        def quantise(z, s0, s1):
+        def weave(copy, z, s0, s1):
+            copy(
+                woven[z][:, PACK * s0 : PACK * s1].rearrange("p (c i j) -> p c j i", i=4, j=PACK),
+                planes[z][:, :, s0 - HALF : s1 - HALF].rearrange("p j (c i) -> p c j i", i=4),
+            )
+
+        def quantise(z, g):
+            s0, s1 = GROUP * g, GROUP * (g + 1)
             nc.vector.quantize_mx(out=codes[z][:, s0:s1].bitcast(FP8X4), scales=scales[z][:, s0:s1], in_=woven[z][:, PACK * s0 : PACK * s1])
 
-        def multiply(z, b, g):
+        def multiply(z, b, g, opens=0):
             s0, s1 = GROUP * g, GROUP * (g + 1)
             nc.tensor.matmul_mx(
                 out=banks[b][g][:],
@@ -105,81 +116,85 @@ def tile_picked_ranknet_sigmoid_e_kernel(tc, xT, w1_words, w1_scales, offs, win,
                 lhsT_scale=w_scales[:, z, P * b : P * (b + 1)],
                 rhs=codes[z][:, s0:s1].bitcast(FP8X4),
                 rhs_scale=scales[z][:, s0:s1],
-                start=(z == 0),
-                stop=(z == PASSES - 1),
+                start=(z == opens),
+                stop=(z != opens),
             )
 
         on_scalar, on_vector = nc.scalar.copy, nc.vector.tensor_copy
 
-        spans = [(GROUP * g, GROUP * (g + 1)) for g in range(GROUPS)]
-
         def copy_out(copy, b, g):
-            copy(y[b][:, spans[g][0] : spans[g][1]], banks[b][g][:])
+            copy(y[b][:, GROUP * g : GROUP * (g + 1)], banks[b][g][:])
 
-        pick(gather_on_scalar, 0, 0, S)
-        pick(gather_on_vector, 1, 0, S)
-        for half in ((0, HALF), (HALF, S)):
-            pick(gather_on_scalar, 2, *half)
-            pick(gather_on_vector, 3, *half)
-        weave_by_lines(on_scalar, *spans[0], 0)
-        weave_by_lines(on_vector, *spans[1], 0)
-        weave_by_lines(on_vector, HALF, S, 0)
-        quantise(0, 0, HALF)
-        quantise(0, HALF, S)
-        pick(gather_on_scalar, 4, 0, S)
-        pick(gather_on_vector, 5, 0, S)
-        pick(gather_on_scalar, 6, 0, 384)
-        pick(gather_on_vector, 6, 384, S)
+        def pick_whole(r):
+            pick_paired(r, 0, 2)
+            pick_plain(r, HALF, S)
 
-        for g in range(GROUPS):
-            pick(gather_on_vector if g < 2 else gather_on_scalar, 7, *spans[g])
-        weave_by_lines(on_vector, *spans[0])
-        weave_by_lines(on_vector, *spans[1])
-        quantise(1, *spans[0])
-        weave_by_lines(on_scalar, *spans[2])
-        weave_by_lines(on_scalar, 384, 448)
-        weave_by_lines(on_vector, 448, S)
-        for g in range(1, GROUPS):
-            quantise(1, *spans[g])
+        def pick_by_groups(r):
+            pick_paired(r, 0, 1)
+            pick_paired(r, 1, 2)
+            pick_plain(r, HALF + GROUP, S)
+            pick_plain(r, HALF, HALF + GROUP)
 
-        for b in range(BLOCKS):
-            for g in range(GROUPS):
-                multiply(0, b, g)
-        for b, g in ((0, 0), (1, 0), (0, 1), (0, 2), (0, 3), (1, 1), (1, 2), (1, 3)):
-            multiply(1, b, g)
-            copy_out(on_vector if (b, g) == (0, 3) else on_scalar, b, g)
+        def close_pass(z):
+            pick_by_groups(PACK * z + PACK - 1)
+            join(z, 0)
+            weave(on_scalar, z, 384, S)
+            join(z, 1)
+            weave(on_vector, z, 256, 352)
+            weave(on_scalar, z, 352, 384)
+            for g in (0, 1, 3, 2):
+                quantise(z, g)
+
+        for r in (0, 1, 2):
+            pick_whole(r)
+        close_pass(0)
+        for r in (4, 5, 6):
+            pick_whole(r)
+        close_pass(1)
 
         lost = [keep.tile([P, V], F32, name="lost%d" % b) for b in range(BLOCKS)]
+        won = keep.tile([P, V // 4], F32, name="won")
         margin = [keep.tile([P, V], F32, name="margin%d" % b) for b in range(BLOCKS)]
         result = [keep.tile([P, V], F32, name="result%d" % b) for b in range(BLOCKS)]
+        first, second = (0, V // 2), (V // 2, V)
 
         def fetch_losers(gather, b, v0, v1):
             gather(lost[b][:, v0:v1], y[b][:], lose_sb, v0, v1)
 
-        def subtract(b, v0, v1):
+        def subtract_fused(b, v0, v1):
             nc.vector.tensor_tensor(margin[b][:, v0:v1], y[b][:].indirect(entries(win_sb, v0, v1)), lost[b][:, v0:v1], SUBTRACT)
 
         def finish(b, v0, v1):
             nc.scalar.activation(result[b][:, v0:v1], margin[b][:, v0:v1], SIGMOID)
             nc.sync.dma_start(out=out[P * b : P * (b + 1), v0:v1], in_=result[b][:, v0:v1])
 
-        first, second = (0, V // 2), (V // 2, V)
-        won = [keep.tile([P, V // 2], F32, name="won%d" % b) for b in range(1)]
+        for g in range(GROUPS):
+            multiply(0, 0, g)
+        for g in (0, 1, 3):
+            multiply(0, 1, g)
+        for g in (0, 1, 3, 2):
+            multiply(1, 0, g)
+            copy_out(on_vector if g == 2 else on_scalar, 0, g)
+        for g in (0, 1, 3):
+            multiply(1, 1, g)
+            copy_out(on_scalar, 1, g)
+        for g in (2,):
+            multiply(1, 1, g, opens=1)
+            multiply(0, 1, g, opens=1)
+            copy_out(on_scalar, 1, g)
+        tail = 192
         fetch_losers(gather_on_vector, 0, *first)
-        fetch_losers(gather_on_scalar, 0, *second)
-        gather_on_vector(won[0][:], y[0][:], win_sb, *second)
+        fetch_losers(gather_on_vector, 0, V // 2, tail)
+        fetch_losers(gather_on_scalar, 0, tail, V)
+        subtract_fused(0, *first)
+        subtract_fused(0, *second)
         fetch_losers(gather_on_scalar, 1, *first)
         fetch_losers(gather_on_scalar, 1, *second)
-        tail = 192
-        won_last = keep.tile([P, V - tail], F32, name="won_last")
-        gather_on_scalar(won_last[:], y[1][:], win_sb, tail, V)
-        subtract(0, *first)
-        nc.vector.tensor_tensor(margin[0][:, V // 2 :], won[0][:], lost[0][:, V // 2 :], SUBTRACT)
+        gather_on_scalar(won[:], y[1][:], win_sb, tail, V)
         finish(0, 0, V)
-        subtract(1, *first)
-        nc.scalar.activation(result[1][:, : V // 2], margin[1][:, : V // 2], SIGMOID)
-        subtract(1, V // 2, tail)
-        nc.scalar.activation(result[1][:, V // 2 : tail], margin[1][:, V // 2 : tail], SIGMOID)
-        nc.vector.tensor_tensor(margin[1][:, tail:], won_last[:], lost[1][:, tail:], SUBTRACT)
-        nc.scalar.activation(result[1][:, tail:], margin[1][:, tail:], SIGMOID)
+        subtract_fused(1, *first)
+        subtract_fused(1, V // 2, tail)
+        nc.vector.tensor_tensor(margin[1][:, tail:], won[:], lost[1][:, tail:], SUBTRACT)
+        for v0, v1 in (first, (V // 2, tail), (tail, V)):
+            nc.scalar.activation(result[1][:, v0:v1], margin[1][:, v0:v1], SIGMOID)
         nc.sync.dma_start(out=out[P:, :], in_=result[1][:])

from contextlib import ExitStack

import concourse.mybir as mybir

K, T, S, V, N = 1024, 1024, 512, 256, 256
FLOPS = 2 * K * N * S

F32 = mybir.dt.float32
BF16 = mybir.dt.bfloat16
I32 = mybir.dt.int32
U32 = mybir.dt.uint32
U16 = mybir.dt.uint16
U8 = mybir.dt.uint8
FP8X4 = mybir.dt.float8_e4m3fn_x4
FP4X4 = mybir.dt.float4_e2m1fn_x4
SIGMOID = mybir.ActivationFunctionType.Sigmoid
COPY = mybir.ActivationFunctionType.Copy
SUBTRACT = mybir.AluOpType.subtract

P = 128
PACK = 4
PASSES = K // (P * PACK)
BLOCKS = N // P
QUADRANT = 32
SCALE_ROWS = 4
LIST_ROWS = 16
GROUP = 128
GROUPS = S // GROUP
HALF = S // 2


def tile_picked_ranknet_sigmoid_e_kernel(tc, xT, w1_words, w1_scales, offs, win, lose, out):
    nc = tc.nc
    x_rows = xT.rearrange("(z p j) t -> z p j t", p=P, j=PACK)

    with ExitStack() as ctx:
        keep = ctx.enter_context(tc.tile_pool(name="keep", bufs=1))
        psum = ctx.enter_context(tc.psum_pool(name="psum", bufs=1))

        offs_sb = keep.tile([P, S // LIST_ROWS], U16, name="offs_sb")
        win_sb = keep.tile([P, V // LIST_ROWS], U16, name="win_sb")
        lose_sb = keep.tile([P, V // LIST_ROWS], U16, name="lose_sb")

        w_scales = keep.tile([P, PASSES, N], U8, name="w_scales", align_bytes=64)
        w_scales_flat = w_scales[:].rearrange("p z n -> p (z n)")
        nc.vector.memset(w_scales_flat.bitcast(I32), 0)
        w_words = [keep.tile([P, 2 * N], U8, name="w_words%d" % z, align_bytes=64) for z in range(PASSES)]

        warm_up = keep.tile([P, 1], F32, name="warm_up")
        nc.scalar.activation(warm_up[:], w_scales_flat.bitcast(F32)[:, 0:1], SIGMOID)

        rows = []
        for source in (x_rows[0, :, 0:2], x_rows[0, :, 2:4], x_rows[1, :, 0:2], x_rows[1, :, 2:3], x_rows[1, :, 3:4]):
            count = source.shape[1]
            loaded = keep.tile([P, count * T], F32, name="loaded%d" % len(rows))
            nc.sync.dma_start(out=loaded[:].rearrange("p (j t) -> p j t", j=count), in_=source)
            if not rows:
                nc.sync.dma_start(offs_sb[:], offs)
            rows.extend([loaded[:, T * i : T * (i + 1)] for i in range(count)])
        for q in range(P // QUADRANT):
            nc.sync.dma_start(
                out=w_scales[QUADRANT * q : QUADRANT * q + SCALE_ROWS].bitcast(I32),
                in_=w1_scales[:, SCALE_ROWS * q : SCALE_ROWS * (q + 1), :].rearrange("z r n -> r z n").bitcast(I32),
            )
        nc.sync.dma_start(out=w_words[0][:], in_=w1_words[0])
        nc.sync.dma_start(out=w_words[1][:], in_=w1_words[1])
        nc.sync.dma_start(lose_sb[:], lose)
        nc.sync.dma_start(win_sb[:], win)

        banks = [[psum.tile([P, GROUP], F32, name="bank%d_%d" % (b, g)) for g in range(GROUPS)] for b in range(BLOCKS)]
        y = [keep.tile([P, S], F32, name="y%d" % b) for b in range(BLOCKS)]
        codes = [keep.tile([P, S], U32, name="codes%d" % z, align_bytes=64) for z in range(PASSES)]
        scales = [keep.tile([P, S], U8, name="scales%d" % z, align_bytes=64) for z in range(PASSES)]
        pairs = [keep.tile([P, 2, 2, GROUP, 2], BF16, name="pairs%d" % z, align_bytes=64) for z in range(PASSES)]
        planes = [keep.tile([P, PACK, HALF], F32, name="planes%d" % z, align_bytes=64) for z in range(PASSES)]
        woven = [keep.tile([P, PACK * S], BF16, name="woven%d" % z, align_bytes=64) for z in range(PASSES)]

        def entries(places, first, end):
            return places[:, first // LIST_ROWS : end // LIST_ROWS]

        def gather_on_scalar(dst, window, places, first, end):
            nc.scalar.activation(dst, window.indirect(entries(places, first, end)), COPY)

        def gather_on_vector(dst, window, places, first, end):
            nc.vector.tensor_copy(dst, window.indirect(entries(places, first, end)))

        def pick_paired(r, g0, g1):
            z, j = divmod(r, PACK)
            gather_on_vector(pairs[z][:, g0:g1, j // 2, :, j % 2], rows[r], offs_sb, GROUP * g0, GROUP * g1)

        def pick_plain(r, s0, s1):
            z, j = divmod(r, PACK)
            gather_on_scalar(planes[z][:, j, s0 - HALF : s1 - HALF], rows[r], offs_sb, s0, s1)

        def join(z, g):
            nc.vector.tensor_copy(
                woven[z][:, PACK * GROUP * g : PACK * GROUP * (g + 1)].bitcast(I32).rearrange("p (s u) -> p s u", u=2),
                pairs[z][:, g].rearrange("p u s e -> p (u s e)").bitcast(I32).rearrange("p (u s) -> p s u", u=2),
            )

        def weave(copy, z, s0, s1):
            copy(
                woven[z][:, PACK * s0 : PACK * s1].rearrange("p (c i j) -> p c j i", i=4, j=PACK),
                planes[z][:, :, s0 - HALF : s1 - HALF].rearrange("p j (c i) -> p c j i", i=4),
            )

        def quantise(z, g):
            s0, s1 = GROUP * g, GROUP * (g + 1)
            nc.vector.quantize_mx(out=codes[z][:, s0:s1].bitcast(FP8X4), scales=scales[z][:, s0:s1], in_=woven[z][:, PACK * s0 : PACK * s1])

        def multiply(z, b, g, opens=0):
            s0, s1 = GROUP * g, GROUP * (g + 1)
            nc.tensor.matmul_mx(
                out=banks[b][g][:],
                lhsT=w_words[z][:, 2 * P * b : 2 * P * (b + 1)].bitcast(FP4X4),
                lhsT_scale=w_scales[:, z, P * b : P * (b + 1)],
                rhs=codes[z][:, s0:s1].bitcast(FP8X4),
                rhs_scale=scales[z][:, s0:s1],
                start=(z == opens),
                stop=(z != opens),
            )

        on_scalar, on_vector = nc.scalar.copy, nc.vector.tensor_copy

        def copy_out(copy, b, g):
            copy(y[b][:, GROUP * g : GROUP * (g + 1)], banks[b][g][:])

        def pick_whole(r):
            pick_paired(r, 0, 2)
            pick_plain(r, HALF, S)

        def pick_by_groups(r):
            pick_paired(r, 0, 1)
            pick_paired(r, 1, 2)
            pick_plain(r, HALF + GROUP, S)
            pick_plain(r, HALF, HALF + GROUP)

        def close_pass(z):
            pick_by_groups(PACK * z + PACK - 1)
            join(z, 0)
            weave(on_scalar, z, 384, S)
            join(z, 1)
            weave(on_vector, z, 256, 352)
            weave(on_scalar, z, 352, 384)
            for g in (0, 1, 3, 2):
                quantise(z, g)

        for r in (0, 1, 2):
            pick_whole(r)
        close_pass(0)
        for r in (4, 5, 6):
            pick_whole(r)
        close_pass(1)

        lost = [keep.tile([P, V], F32, name="lost%d" % b) for b in range(BLOCKS)]
        won = keep.tile([P, V // 4], F32, name="won")
        margin = [keep.tile([P, V], F32, name="margin%d" % b) for b in range(BLOCKS)]
        result = [keep.tile([P, V], F32, name="result%d" % b) for b in range(BLOCKS)]
        first, second = (0, V // 2), (V // 2, V)

        def fetch_losers(gather, b, v0, v1):
            gather(lost[b][:, v0:v1], y[b][:], lose_sb, v0, v1)

        def subtract_fused(b, v0, v1):
            nc.vector.tensor_tensor(margin[b][:, v0:v1], y[b][:].indirect(entries(win_sb, v0, v1)), lost[b][:, v0:v1], SUBTRACT)

        def finish(b, v0, v1):
            nc.scalar.activation(result[b][:, v0:v1], margin[b][:, v0:v1], SIGMOID)
            nc.sync.dma_start(out=out[P * b : P * (b + 1), v0:v1], in_=result[b][:, v0:v1])

        for g in range(GROUPS):
            multiply(0, 0, g)
        for g in (0, 1, 3):
            multiply(0, 1, g)
        for g in (0, 1, 3, 2):
            multiply(1, 0, g)
            copy_out(on_vector if g == 2 else on_scalar, 0, g)
        for g in (0, 1, 3):
            multiply(1, 1, g)
            copy_out(on_scalar, 1, g)
        for g in (2,):
            multiply(1, 1, g, opens=1)
            multiply(0, 1, g, opens=1)
            copy_out(on_scalar, 1, g)
        tail = 192
        fetch_losers(gather_on_vector, 0, *first)
        fetch_losers(gather_on_vector, 0, V // 2, tail)
        fetch_losers(gather_on_scalar, 0, tail, V)
        subtract_fused(0, *first)
        subtract_fused(0, *second)
        fetch_losers(gather_on_scalar, 1, *first)
        fetch_losers(gather_on_scalar, 1, *second)
        gather_on_scalar(won[:], y[1][:], win_sb, tail, V)
        finish(0, 0, V)
        subtract_fused(1, *first)
        subtract_fused(1, V // 2, tail)
        nc.vector.tensor_tensor(margin[1][:, tail:], won[:], lost[1][:, tail:], SUBTRACT)
        for v0, v1 in (first, (V // 2, tail), (tail, V)):
            nc.scalar.activation(result[1][:, v0:v1], margin[1][:, v0:v1], SIGMOID)
        nc.sync.dma_start(out=out[P:, :], in_=result[1][:])
